import numpy as np
import ml_dtypes


def mxq(x, axis, fmt="e4m3"):
    dtype, down = {"e4m3": (ml_dtypes.float8_e4m3fn, 7), "e5m2": (ml_dtypes.float8_e5m2, 14)}[fmt]
    v = np.moveaxis(np.asarray(x, np.float32).astype(ml_dtypes.bfloat16).astype(np.float64), axis, -1)
    blocks = v.reshape(v.shape[:-1] + (-1, 32))
    amax = np.abs(blocks).max(-1, keepdims=True)
    byte = np.maximum(np.where(amax > 0, np.frexp(amax)[1] - 1 + 127, 0) - down, 1)
    scale = np.exp2(byte - 127.0)
    codes = (blocks / scale).astype(np.float32).astype(dtype).astype(np.float64)
    return np.moveaxis((codes * scale).reshape(v.shape), -1, axis)


WIDE = False


def mx_kscale(k):
    if not WIDE:
        return np.ones(k)
    levels = np.array([10, -10, 5, -5, 0])
    if k % 512:
        return np.exp2(np.random.permutation(np.resize(levels, k // 32))).repeat(32)
    a = np.empty((k // 512, 16))
    for p in range(k // 512):
        a[p, :8] = np.random.permutation(np.resize(levels, 8))
        for g in range(8):
            far = levels[np.abs(levels - a[p, g]) >= 10]
            a[p, g + 8] = far[np.random.randint(len(far))]
    return np.exp2(a.ravel()).repeat(32)


BF16 = ml_dtypes.bfloat16


def bf(x):
    return np.asarray(x, np.float32).astype(BF16)


def f64(x):
    return np.asarray(x).astype(np.float64)


E2M1 = np.array([0.0, 0.5, 1.0, 1.5, 2.0, 3.0, 4.0, 6.0, -0.0, -0.5, -1.0, -1.5, -2.0, -3.0, -4.0, -6.0])


def pack_weight(w, fmt):
    k, n = w.shape
    w = f64(bf(w)).reshape(k // 32, 32, n)
    amax = np.abs(w).max(1)
    if fmt == "e4m3":
        byte = np.frexp(amax)[1] - 1 + 127 - 7
    else:
        mant, ex = np.frexp(amax / 6.0)
        byte = np.where(mant > 0.5, ex, ex - 1) + 127
    byte = np.clip(np.where(amax > 0, byte, 1), 1, 254)
    scaled = (w * np.exp2(127.0 - byte)[:, None, :]).reshape(k, n).astype(np.float32)
    by_word = np.ascontiguousarray(scaled.reshape(k // 512, 128, 4, n).transpose(0, 1, 3, 2))
    if fmt == "e4m3":
        words = by_word.astype(ml_dtypes.float8_e4m3fn).view(np.uint8)
    else:
        c = by_word.astype(ml_dtypes.float4_e2m1fn).view(np.uint8) & 0xF
        words = c[..., 0::2] | (c[..., 1::2] << 4)
    return np.ascontiguousarray(words), np.ascontiguousarray(byte.astype(np.uint8).reshape(k // 512, 16, n))


def unpack_weight(words, scales, fmt):
    g, p, n, _ = words.shape
    if fmt == "e4m3":
        vals = np.ascontiguousarray(words).view(ml_dtypes.float8_e4m3fn).astype(np.float64)
    else:
        nib = np.empty((g, p, n, 4), np.uint8)
        nib[..., 0::2] = words & 0xF
        nib[..., 1::2] = words >> 4
        vals = E2M1[nib]
    vals = vals * np.repeat(np.exp2(scales.astype(np.float64) - 127.0), 8, axis=1)[..., None]
    return vals.transpose(0, 1, 3, 2).reshape(g * 512, n)
def pack4(w):
    words, scales = pack_weight(w, "e2m1")
    return words.reshape(words.shape[0], 128, -1), scales


def unpack4(words, scales):
    return unpack_weight(words.reshape(words.shape[0], 128, -1, 2), scales, "e2m1")


N, D, P, G, H = 1024, 1024, 512, 512, 1024


def sigmoid(v):
    return 1.0 / (1.0 + np.exp(-v))


def draw0():
    s, u, t = mx_kscale(D), mx_kscale(P), mx_kscale(G)
    x = bf(np.random.standard_normal((N, D)) * s)
    prior = bf(np.random.standard_normal((N, P)) * u)
    wx_words, wx_scales = pack4(np.random.standard_normal((D, G)) / np.sqrt(D) / s[:, None] * t)
    wp_words, wp_scales = pack4(np.random.standard_normal((P, G)) / np.sqrt(P) / u[:, None] * t)
    b1 = bf(np.random.standard_normal(G) * 0.5 * t)
    w2_words, w2_scales = pack4(np.random.standard_normal((G, H)) / np.sqrt(G) / t[:, None])
    wl_words, wl_scales = pack4(np.random.standard_normal((D, H)) / np.sqrt(D) / s[:, None])
    return {
        "x": x,
        "prior": prior,
        "wx_words": wx_words,
        "wx_scales": wx_scales,
        "wp_words": wp_words,
        "wp_scales": wp_scales,
        "b1": b1,
        "w2_words": w2_words,
        "w2_scales": w2_scales,
        "wl_words": wl_words,
        "wl_scales": wl_scales,
    }


def core(x, prior, wx_words, wx_scales, wp_words, wp_scales, b1, w2_words, w2_scales, wl_words, wl_scales):
    xq = mxq(f64(x), 1, "e4m3")
    pq = mxq(f64(prior), 1, "e4m3")
    a = (pq @ unpack4(wp_words, wp_scales)) + (xq @ unpack4(wx_words, wx_scales)) + f64(b1)[None, :]
    r = np.maximum(a, 0.0)
    t = mxq(r, 1, "e4m3") @ unpack4(w2_words, w2_scales)
    gate = 2.0 * sigmoid(t)
    h = np.maximum(xq @ unpack4(wl_words, wl_scales), 0.0)
    return gate * h


def e4m3fn_bytes(y):
    return np.clip(np.asarray(y, np.float64), -448.0, 448.0).astype(np.float32).astype(ml_dtypes.float8_e4m3fn).view(np.uint8)


def e4m3fn_values(b):
    return np.asarray(b, np.uint8).view(ml_dtypes.float8_e4m3fn).astype(np.float64)


def setup_inputs():
    d = draw0()
    x0 = np.asarray(d['x']).astype(np.float64)
    s = (np.max(np.abs(x0), axis=(0,), keepdims=True) / 448.0).astype(np.float32)
    out = {}
    for k, v in d.items():
        if k == 'x':
            out['x_bytes'] = e4m3fn_bytes(x0 / s.astype(np.float64))
            out['x_scale'] = s
        else:
            out[k] = v
    return out


def reference(x_bytes, x_scale, prior, wx_words, wx_scales, wp_words, wp_scales, b1, w2_words, w2_scales, wl_words, wl_scales):
    return core(e4m3fn_values(x_bytes) * x_scale.astype(np.float64), prior, wx_words, wx_scales, wp_words, wp_scales, b1, w2_words, w2_scales, wl_words, wl_scales)

@@ -1,0 +1,306 @@
+from contextlib import ExitStack
+
+import concourse.mybir as mybir
+from concourse.masks import make_identity
+
+P = 128
+TOKENS, D, PRIOR, G, HID = 1024, 1024, 512, 512, 1024
+NT = TOKENS // P
+PAIRS = NT // 2
+BANK = 512
+FLOPS = 2 * TOKENS * (D * G + PRIOR * G + G * HID + D * HID)
+
+F32 = mybir.dt.float32
+BF16 = mybir.dt.bfloat16
+I32 = mybir.dt.int32
+U32 = mybir.dt.uint32
+U8 = mybir.dt.uint8
+FP8 = mybir.dt.float8_e4m3fn
+FP8X4 = mybir.dt.float8_e4m3fn_x4
+FP4X4 = mybir.dt.float4_e2m1fn_x4
+ACT = mybir.ActivationFunctionType
+ALU = mybir.AluOpType
+
+
+def tile_pepnetpriorgatedhiddenlayer_w4_kernel(
+    tc, x_bytes, x_scale, prior, wx_words, wx_scales, wp_words, wp_scales, b1, w2_words, w2_scales, wl_words, wl_scales, out
+):
+    nc = tc.nc
+    with ExitStack() as ctx:
+        keep = ctx.enter_context(tc.tile_pool(name="keep", bufs=1))
+        work = ctx.enter_context(tc.tile_pool(name="work", bufs=3))
+        psum = ctx.enter_context(tc.psum_pool(name="psum", bufs=1))
+
+        warm = keep.tile([P, BANK], BF16)
+        nc.vector.memset(warm[:], 0.0)
+        dummy = keep.tile([P, 1], F32)
+        nc.vector.memset(dummy[:], 0.0)
+        nc.scalar.activation(out=dummy[:], in_=dummy[:], func=ACT.Sigmoid)
+        ident = keep.tile([P, P], F32)
+        make_identity(nc, ident[:])
+        ident_bf = keep.tile([P, P], BF16)
+        nc.gpsimd.tensor_copy(out=ident_bf[:], in_=ident[:])
+
+        a_scales = keep.tile([P, 3, G], U8, align_bytes=64)
+        w2_sc = keep.tile([P, HID], U8, align_bytes=64)
+        wl_sc = keep.tile([P, 2, HID], U8, align_bytes=64)
+        nc.vector.memset(a_scales[:].rearrange("p c n -> p (c n)").bitcast(I32), 0)
+        nc.vector.memset(w2_sc[:].bitcast(I32), 0)
+        nc.vector.memset(wl_sc[:].rearrange("p c n -> p (c n)").bitcast(I32), 0)
+
+        s_col = keep.tile([P, 2, 4], F32)
+        nc.sync.dma_start(out=s_col[:], in_=x_scale.rearrange("o (j p m) -> p (o j) m", j=2, m=4))
+
+        x_rows = x_bytes.rearrange("(p n) k -> p n k", n=NT)
+        prior_rows = prior.rearrange("(p n) k -> p n k", n=NT)
+        out_rows = out.rearrange("(p n) h -> p n h", n=NT)
+        x_fp8, prior_in = [None] * PAIRS, [None] * PAIRS
+
+        def load_x(q):
+            x_fp8[q] = keep.tile([P, 2, D], U8, name="x_fp8_%d" % q)
+            nc.sync.dma_start(out=x_fp8[q][:], in_=x_rows[:, 2 * q : 2 * q + 2, :])
+
+        def load_prior(q, engine):
+            prior_in[q] = keep.tile([P, 2, PRIOR], BF16, name="prior_in_%d" % q)
+            engine.dma_start(out=prior_in[q][:], in_=prior_rows[:, 2 * q : 2 * q + 2, :])
+
+        def load_scales(scale_tile, src):
+            for quad in range(4):
+                nc.sync.dma_start(
+                    out=scale_tile[32 * quad : 32 * quad + 4, :, :].bitcast(I32),
+                    in_=src[:, 4 * quad : 4 * quad + 4, :].rearrange("g q n -> q g n").bitcast(I32),
+                )
+
+        load_x(0)
+        load_prior(0, nc.scalar)
+        load_x(1)
+        load_prior(1, nc.scalar)
+        load_scales(a_scales[:, 1:3, :], wx_scales)
+        wx = keep.tile([P, 2, 2 * G], U8, align_bytes=64)
+        nc.sync.dma_start(out=wx[:].bitcast(I32), in_=wx_words.rearrange("g p b -> p g b").bitcast(I32))
+        wp = keep.tile([P, 1, 2 * G], U8, align_bytes=64)
+        nc.sync.dma_start(out=wp[:].bitcast(I32), in_=wp_words.rearrange("g p b -> p g b").bitcast(I32))
+        load_scales(a_scales[:, 0:1, :], wp_scales)
+        b_col = keep.tile([P, 4], BF16)
+        nc.sync.dma_start(out=b_col[:], in_=b1.rearrange("(p m) -> p m", m=4))
+        load_scales(w2_sc[:].rearrange("p (c n) -> p c n", c=1), w2_scales)
+        load_scales(wl_sc, wl_scales)
+        w2 = keep.tile([P, 1, 2 * HID], U8, align_bytes=64)
+        nc.sync.dma_start(out=w2[:].bitcast(I32), in_=w2_words.rearrange("g p b -> p g b").bitcast(I32))
+        load_x(2)
+        wl = keep.tile([P, 2, 2 * HID], U8, align_bytes=64)
+        nc.sync.dma_start(out=wl[:].bitcast(I32), in_=wl_words.rearrange("g p b -> p g b").bitcast(I32))
+        load_prior(2, nc.sync)
+        load_x(3)
+        load_prior(3, nc.sync)
+
+        s_all = keep.tile([P, D], F32)
+        bias = keep.tile([P, 2, P, 2], F32)
+
+        def spread_scales():
+            for j in range(2):
+                spread = psum.tile([P, 4, P], F32, name="spread%d" % j, tag="tr", bufs=2)
+                for m in range(4):
+                    nc.tensor.transpose(spread[:, m, :], s_col[:, j, m : m + 1].to_broadcast([P, P]), ident[:])
+                for p0, p1 in ((0, P // 2), (P // 2, P)) if j == 0 else ((0, P),):
+                    nc.scalar.activation(
+                        out=s_all[:, 512 * j + 4 * p0 : 512 * j + 4 * p1].rearrange("c (p m) -> c p m", m=4),
+                        in_=spread[:, :, p0:p1].rearrange("c m p -> c p m"),
+                        func=ACT.Copy,
+                        scale=2.0,
+                    )
+
+        def spread_bias():
+            spread_b = psum.tile([P, 4, P], BF16, tag="r", bufs=1)
+            for m in range(4):
+                nc.tensor.transpose(spread_b[:, m, :], b_col[:, m : m + 1].to_broadcast([P, P]), ident_bf[:])
+            nc.scalar.activation(
+                out=bias[:], in_=spread_b[:].rearrange("c (u e) p -> c u p e", u=2), func=ACT.Copy, scale=2.0
+            )
+
+        prior_t, prior_grouped, prior_codes, prior_mx_scales = {}, {}, {}, {}
+
+        def transpose_prior(q):
+            prior_t[q] = psum.tile([P, 2, 2, P], F32, name="prior_t%d" % q, tag="h" if q == 1 else "tr", bufs=2)
+            words = prior_in[q][:].rearrange("p n k -> p (n k)").bitcast(F32)
+            for i in range(2):
+                for u in range(2):
+                    nc.tensor.transpose(prior_t[q][:, i, u, :], words[:, 256 * i + u : 256 * (i + 1) : 2], ident[:])
+
+        def copy_prior(q):
+            prior_grouped[q] = work.tile([P, 2 * P * 4], BF16, name="prior_grouped%d" % q, tag="prior_grouped", bufs=2, align_bytes=64)
+            for i in range(2):
+                nc.scalar.activation(
+                    out=prior_grouped[q][:, 512 * i : 512 * (i + 1)].rearrange("p (r u e) -> p r u e", u=2, e=2),
+                    in_=prior_t[q][:, i, :, :].rearrange("p u r -> p (u r)").bitcast(BF16).rearrange("p (u r e) -> p r u e", u=2, e=2),
+                    func=ACT.Copy,
+                    scale=2.0,
+                )
+
+        def quantize_prior(q):
+            prior_codes[q] = keep.tile([P, 2 * P], U32, name="prior_codes%d" % q, align_bytes=64)
+            prior_mx_scales[q] = keep.tile([P, 2 * P], U8, name="prior_mx_scales%d" % q, align_bytes=64)
+            nc.vector.quantize_mx(out=prior_codes[q][:].bitcast(FP8X4), scales=prior_mx_scales[q][:], in_=prior_grouped[q][:])
+
+        x_scaled, x_t, x_grouped, x_codes, x_mx_scales = {}, {}, {}, {}, {}
+
+        def scale_x(n):
+            x_scaled[n] = work.tile([P, D], BF16, name="x_scaled%d" % n, tag="x_scaled", bufs=3)
+            for c0, c1 in ((0, 256), (256, 512), (512, 1024)) if n == 0 else ((0, 1024),):
+                nc.vector.tensor_tensor(
+                    out=x_scaled[n][:, c0:c1], in0=x_fp8[n // 2][:, n % 2, c0:c1].bitcast(FP8), in1=s_all[:, c0:c1], op=ALU.mult
+                )
+
+        def transpose_x(n):
+            x_t[n] = psum.tile([P, 2, 2, P], F32, name="x_t%d" % n, tag="tr", bufs=2)
+            words = x_scaled[n][:].bitcast(F32)
+            for g in range(2):
+                for u in range(2):
+                    nc.tensor.transpose(x_t[n][:, g, u, :], words[:, 256 * g + u : 256 * (g + 1) : 2], ident[:])
+
+        def copy_x(n):
+            x_grouped[n] = work.tile([P, 2 * P * 4], BF16, name="x_grouped%d" % n, tag="x_grouped", bufs=3, align_bytes=64)
+            nc.scalar.copy(
+                out=x_grouped[n][:].bitcast(F32).rearrange("p (g r u) -> p g r u", g=2, u=2),
+                in_=x_t[n][:].rearrange("p g u r -> p g r u"),
+            )
+
+        def quantize_x(n):
+            x_codes[n] = keep.tile([P, 2 * P], U32, name="x_codes%d" % n, align_bytes=64)
+            x_mx_scales[n] = keep.tile([P, 2 * P], U8, name="x_mx_scales%d" % n, align_bytes=64)
+            nc.vector.quantize_mx(out=x_codes[n][:].bitcast(FP8X4), scales=x_mx_scales[n][:], in_=x_grouped[n][:])
+
+        acc_a, r_rows, r_t, r_grouped, r_codes, r_mx_scales = {}, {}, {}, {}, {}, {}
+
+        def matmul_a(n):
+            acc_a[n] = psum.tile([P, G], F32, name="acc_a%d" % n, tag="a", bufs=1)
+            c0 = P * (n % 2)
+            for i in range(3):
+                if i == 0:
+                    codes, scales, w = prior_codes[n // 2][:, c0 : c0 + P], prior_mx_scales[n // 2][:, c0 : c0 + P], wp[:, 0, :]
+                else:
+                    codes, scales, w = x_codes[n][:, P * (i - 1) : P * i], x_mx_scales[n][:, P * (i - 1) : P * i], wx[:, i - 1, :]
+                nc.tensor.matmul_mx(
+                    out=acc_a[n][:], lhsT=codes.bitcast(FP8X4), lhsT_scale=scales, rhs=w.bitcast(FP4X4),
+                    rhs_scale=a_scales[:, i, :], start=(i == 0), stop=(i == 2),
+                )
+
+        def add_bias(n):
+            r_rows[n] = work.tile([P, 2, P, 2], BF16, name="r_rows%d" % n, tag="r_rows", bufs=2)
+            nc.vector.tensor_tensor(
+                out=r_rows[n][:], in0=acc_a[n][:].rearrange("c (p u e) -> c u p e", u=2, e=2), in1=bias[:], op=ALU.add
+            )
+
+        def transpose_r(n):
+            r_t[n] = psum.tile([P, 2 * P], F32, name="r_t%d" % n, tag="r", bufs=1)
+            words = r_rows[n][:].rearrange("c u p e -> c (u p e)").bitcast(F32)
+            for u in range(2):
+                nc.tensor.transpose(r_t[n][:, P * u : P * (u + 1)], words[:, P * u : P * (u + 1)], ident[:])
+
+        def relu_r(n):
+            r_grouped[n] = work.tile([P, P * 4], BF16, name="r_grouped%d" % n, tag="r_grouped", bufs=2, align_bytes=64)
+            nc.scalar.activation(
+                out=r_grouped[n][:].rearrange("p (c u e) -> p c u e", u=2, e=2),
+                in_=r_t[n][:].bitcast(BF16).rearrange("p (u c e) -> p c u e", u=2, e=2),
+                func=ACT.Relu,
+            )
+
+        def quantize_r(n):
+            r_codes[n] = work.tile([P, P], U32, name="r_codes%d" % n, tag="r_codes", bufs=3, align_bytes=64)
+            r_mx_scales[n] = work.tile([P, P], U8, name="r_mx_scales%d" % n, tag="r_mx_scales", bufs=3, align_bytes=64)
+            nc.vector.quantize_mx(out=r_codes[n][:].bitcast(FP8X4), scales=r_mx_scales[n][:], in_=r_grouped[n][:])
+
+        acc_t, acc_h, gate, res = {}, {}, {}, {}
+
+        def matmul_t(n, j):
+            acc_t[n, j] = psum.tile([P, BANK], F32, name="acc_t%d_%d" % (n, j), tag="t", bufs=2)
+            nc.tensor.matmul_mx(
+                out=acc_t[n, j][:], lhsT=r_codes[n][:].bitcast(FP8X4), lhsT_scale=r_mx_scales[n][:],
+                rhs=w2[:, 0, 2 * BANK * j : 2 * BANK * (j + 1)].bitcast(FP4X4), rhs_scale=w2_sc[:, BANK * j : BANK * (j + 1)],
+                start=True, stop=True,
+            )
+
+        def sigmoid_t(n, j):
+            gate[n, j] = work.tile([P, BANK], F32, name="gate%d_%d" % (n, j), tag="gate", bufs=6)
+            nc.scalar.activation(out=gate[n, j][:], in_=acc_t[n, j][:], func=ACT.Sigmoid, scale=0.5)
+
+        def matmul_h(n, j):
+            acc_h[n, j] = psum.tile([P, BANK], F32, name="acc_h%d_%d" % (n, j), tag="h", bufs=2)
+            for g in range(2):
+                nc.tensor.matmul_mx(
+                    out=acc_h[n, j][:], lhsT=x_codes[n][:, P * g : P * (g + 1)].bitcast(FP8X4), lhsT_scale=x_mx_scales[n][:, P * g : P * (g + 1)],
+                    rhs=wl[:, g, 2 * BANK * j : 2 * BANK * (j + 1)].bitcast(FP4X4), rhs_scale=wl_sc[:, g, BANK * j : BANK * (j + 1)],
+                    start=(g == 0), stop=(g == 1),
+                )
+
+        def gate_and_store(n, j):
+            if j == 0:
+                res[n] = work.tile([P, HID], F32, name="res%d" % n, tag="res", bufs=3)
+            nc.vector.scalar_tensor_tensor(
+                out=res[n][:, BANK * j : BANK * (j + 1)], in0=acc_h[n, j][:], scalar=0.0, in1=gate[n, j][:], op0=ALU.max, op1=ALU.mult
+            )
+            if n == NT - 1:
+                nc.sync.dma_start(out=out_rows[:, n, BANK * j : BANK * (j + 1)], in_=res[n][:, BANK * j : BANK * (j + 1)])
+            elif j == 1:
+                nc.sync.dma_start(out=out_rows[:, n, :], in_=res[n][:])
+
+        def keep_tensor_busy(count):
+            for i in range(count):
+                junk = psum.tile([P, BANK], F32, name="junk", tag="t", bufs=2)
+                nc.tensor.matmul(junk[:], warm[:, 0:P], warm[:], start=True, stop=True)
+
+        def both_halves(stage, n):
+            for j in range(2):
+                stage(n, j)
+
+        ctx.enter_context(tc.manual_schedule())
+        keep_tensor_busy(3)
+        spread_scales()
+        transpose_prior(0)
+        copy_prior(0)
+        keep_tensor_busy(3)
+        scale_x(0)
+        transpose_x(0)
+        copy_x(0)
+        scale_x(1)
+        quantize_prior(0)
+        transpose_prior(1)
+        transpose_x(1)
+        copy_x(1)
+        quantize_x(0)
+        spread_bias()
+        copy_prior(1)
+        matmul_a(0)
+        scale_x(2)
+        add_bias(0)
+        quantize_x(1)
+        scale_x(3)
+        for i in range(NT + 1):
+            if i + 2 < NT:
+                transpose_x(i + 2)
+                copy_x(i + 2)
+            if i < NT:
+                transpose_r(i)
+                relu_r(i)
+            if i % 2 == 1 and (i + 3) // 2 < PAIRS:
+                transpose_prior((i + 3) // 2)
+                copy_prior((i + 3) // 2)
+            if i > 0:
+                both_halves(matmul_t, i - 1)
+                both_halves(sigmoid_t, i - 1)
+            if i + 1 < NT:
+                matmul_a(i + 1)
+            if i > 0:
+                both_halves(matmul_h, i - 1)
+            if i + 1 < NT:
+                add_bias(i + 1)
+            if i < NT:
+                quantize_r(i)
+            if i % 2 == 0 and (i + 2) // 2 < PAIRS:
+                quantize_prior((i + 2) // 2)
+            if i + 2 < NT:
+                quantize_x(i + 2)
+            if i > 0:
+                both_halves(gate_and_store, i - 1)
+            if i + 4 < NT:
+                scale_x(i + 4)

@@ -6,7 +6,6 @@ from concourse.masks import make_identity
 P = 128
 TOKENS, D, PRIOR, G, HID = 1024, 1024, 512, 512, 1024
 NT = TOKENS // P
-PAIRS = NT // 2
 BANK = 512
 FLOPS = 2 * TOKENS * (D * G + PRIOR * G + G * HID + D * HID)
 
@@ -30,39 +29,42 @@ def tile_pepnetpriorgatedhiddenlayer_w4_kernel(
         keep = ctx.enter_context(tc.tile_pool(name="keep", bufs=1))
         work = ctx.enter_context(tc.tile_pool(name="work", bufs=3))
         psum = ctx.enter_context(tc.psum_pool(name="psum", bufs=1))
+        ctx.enter_context(tc.manual_schedule())
 
-        warm = keep.tile([P, BANK], BF16)
-        nc.vector.memset(warm[:], 0.0)
-        dummy = keep.tile([P, 1], F32)
-        nc.vector.memset(dummy[:], 0.0)
-        nc.scalar.activation(out=dummy[:], in_=dummy[:], func=ACT.Sigmoid)
-        ident = keep.tile([P, P], F32)
+        two = keep.tile([P, 1], F32, name="two")
+        nc.gpsimd.memset(two[:], 2.0)
+        ident = keep.tile([P, P], F32, name="ident")
         make_identity(nc, ident[:])
-        ident_bf = keep.tile([P, P], BF16)
-        nc.gpsimd.tensor_copy(out=ident_bf[:], in_=ident[:])
+        twos = keep.tile([P, BANK], BF16, name="twos")
+        nc.vector.memset(twos[:], 2.0)
+        table_out = keep.tile([P, 1], F32, name="table_out")
+        nc.scalar.activation(out=table_out[:], in_=two[:], func=ACT.Sigmoid)
+        b_row = keep.tile([P, G], BF16, name="b_row")
 
-        a_scales = keep.tile([P, 3, G], U8, align_bytes=64)
-        w2_sc = keep.tile([P, HID], U8, align_bytes=64)
-        wl_sc = keep.tile([P, 2, HID], U8, align_bytes=64)
+        a_scales = keep.tile([P, 3, G], U8, name="a_scales", align_bytes=64)
+        w2_sc = keep.tile([P, 1, HID], U8, name="w2_sc", align_bytes=64)
+        wl_sc = keep.tile([P, 2, HID], U8, name="wl_sc", align_bytes=64)
         nc.vector.memset(a_scales[:].rearrange("p c n -> p (c n)").bitcast(I32), 0)
-        nc.vector.memset(w2_sc[:].bitcast(I32), 0)
-        nc.vector.memset(wl_sc[:].rearrange("p c n -> p (c n)").bitcast(I32), 0)
-
-        s_col = keep.tile([P, 2, 4], F32)
-        nc.sync.dma_start(out=s_col[:], in_=x_scale.rearrange("o (j p m) -> p (o j) m", j=2, m=4))
+        nc.vector.memset(b_row[:], 0.0)
+        for plane in (wl_sc, w2_sc):
+            nc.vector.memset(plane[:].rearrange("p c n -> p (c n)").bitcast(I32), 0)
 
         x_rows = x_bytes.rearrange("(p n) k -> p n k", n=NT)
         prior_rows = prior.rearrange("(p n) k -> p n k", n=NT)
         out_rows = out.rearrange("(p n) h -> p n h", n=NT)
-        x_fp8, prior_in = [None] * PAIRS, [None] * PAIRS
+        x_fp8, prior_in = {}, {}
 
-        def load_x(q):
-            x_fp8[q] = keep.tile([P, 2, D], U8, name="x_fp8_%d" % q)
-            nc.sync.dma_start(out=x_fp8[q][:], in_=x_rows[:, 2 * q : 2 * q + 2, :])
+        def load_x(n0, n1):
+            rows = keep.tile([P, n1 - n0, D], U8, name="x_fp8_%d" % n0)
+            nc.sync.dma_start(out=rows[:], in_=x_rows[:, n0:n1, :])
+            for n in range(n0, n1):
+                x_fp8[n] = rows[:, n - n0, :].bitcast(FP8)
 
-        def load_prior(q, engine):
-            prior_in[q] = keep.tile([P, 2, PRIOR], BF16, name="prior_in_%d" % q)
-            engine.dma_start(out=prior_in[q][:], in_=prior_rows[:, 2 * q : 2 * q + 2, :])
+        def load_prior(n0, n1):
+            rows = keep.tile([P, (n1 - n0) * PRIOR], BF16, name="prior_in_%d" % n0)
+            nc.sync.dma_start(out=rows[:], in_=prior_rows[:, n0:n1, :].rearrange("p n k -> p (n k)"))
+            for n in range(n0, n1):
+                prior_in[n] = rows[:, (n - n0) * PRIOR : (n - n0 + 1) * PRIOR]
 
         def load_scales(scale_tile, src):
             for quad in range(4):
@@ -71,118 +73,148 @@ def tile_pepnetpriorgatedhiddenlayer_w4_kernel(
                     in_=src[:, 4 * quad : 4 * quad + 4, :].rearrange("g q n -> q g n").bitcast(I32),
                 )
 
-        load_x(0)
-        load_prior(0, nc.scalar)
-        load_x(1)
-        load_prior(1, nc.scalar)
+        def load_words(name, src):
+            words = keep.tile([P, src.shape[0], src.shape[2]], U8, name=name, align_bytes=64)
+            nc.sync.dma_start(out=words[:].bitcast(I32), in_=src.rearrange("g p b -> p g b").bitcast(I32))
+            return words
+
+        load_x(0, 1)
+        s_col = keep.tile([P, 2, 4], F32, name="s_col")
+        nc.sync.dma_start(out=s_col[:], in_=x_scale.rearrange("o (g p m) -> p (o g) m", g=2, m=4))
+        load_x(1, 2)
+        load_prior(0, 2)
         load_scales(a_scales[:, 1:3, :], wx_scales)
-        wx = keep.tile([P, 2, 2 * G], U8, align_bytes=64)
-        nc.sync.dma_start(out=wx[:].bitcast(I32), in_=wx_words.rearrange("g p b -> p g b").bitcast(I32))
-        wp = keep.tile([P, 1, 2 * G], U8, align_bytes=64)
-        nc.sync.dma_start(out=wp[:].bitcast(I32), in_=wp_words.rearrange("g p b -> p g b").bitcast(I32))
+        wx = load_words("wx", wx_words)
+        nc.sync.dma_start(out=b_row[0:1, :], in_=b1.rearrange("(o n) -> o n", o=1))
+        load_x(2, 3)
         load_scales(a_scales[:, 0:1, :], wp_scales)
-        b_col = keep.tile([P, 4], BF16)
-        nc.sync.dma_start(out=b_col[:], in_=b1.rearrange("(p m) -> p m", m=4))
-        load_scales(w2_sc[:].rearrange("p (c n) -> p c n", c=1), w2_scales)
+        wp = load_words("wp", wp_words)
         load_scales(wl_sc, wl_scales)
-        w2 = keep.tile([P, 1, 2 * HID], U8, align_bytes=64)
-        nc.sync.dma_start(out=w2[:].bitcast(I32), in_=w2_words.rearrange("g p b -> p g b").bitcast(I32))
-        load_x(2)
-        wl = keep.tile([P, 2, 2 * HID], U8, align_bytes=64)
-        nc.sync.dma_start(out=wl[:].bitcast(I32), in_=wl_words.rearrange("g p b -> p g b").bitcast(I32))
-        load_prior(2, nc.sync)
-        load_x(3)
-        load_prior(3, nc.sync)
+        wl = [load_words("wl0", wl_words[:, :, 0 : 2 * BANK])]
+        load_x(3, 4)
+        wl.append(load_words("wl1", wl_words[:, :, 2 * BANK : 4 * BANK]))
+        load_prior(2, 4)
+        load_scales(w2_sc, w2_scales)
+        w2 = load_words("w2", w2_words)
+        load_x(4, 6)
+        load_prior(4, 6)
+        load_x(6, 8)
+        load_prior(6, 8)
 
-        s_all = keep.tile([P, D], F32)
-        bias = keep.tile([P, 2, P, 2], F32)
+        s_twice = keep.tile([P, 2, 4], F32, name="s_twice")
+        bias = keep.tile([P, 2, P, 2], F32, name="bias")
 
-        def spread_scales():
-            for j in range(2):
-                spread = psum.tile([P, 4, P], F32, name="spread%d" % j, tag="tr", bufs=2)
-                for m in range(4):
-                    nc.tensor.transpose(spread[:, m, :], s_col[:, j, m : m + 1].to_broadcast([P, P]), ident[:])
-                for p0, p1 in ((0, P // 2), (P // 2, P)) if j == 0 else ((0, P),):
-                    nc.scalar.activation(
-                        out=s_all[:, 512 * j + 4 * p0 : 512 * j + 4 * p1].rearrange("c (p m) -> c p m", m=4),
-                        in_=spread[:, :, p0:p1].rearrange("c m p -> c p m"),
-                        func=ACT.Copy,
-                        scale=2.0,
-                    )
+        def double_scales():
+            nc.vector.tensor_scalar(out=s_twice[:], in0=s_col[:], scalar1=2.0, scalar2=None, op0=ALU.mult)
 
         def spread_bias():
-            spread_b = psum.tile([P, 4, P], BF16, tag="r", bufs=1)
-            for m in range(4):
-                nc.tensor.transpose(spread_b[:, m, :], b_col[:, m : m + 1].to_broadcast([P, P]), ident_bf[:])
-            nc.scalar.activation(
-                out=bias[:], in_=spread_b[:].rearrange("c (u e) p -> c u p e", u=2), func=ACT.Copy, scale=2.0
-            )
+            spread = new_bank("spread", "t0")
+            nc.tensor.matmul(spread[:], twos[:, 0:P], b_row[:], start=True, stop=True)
+            return spread
+
+        def copy_bias(spread):
+            nc.scalar.copy(out=bias[:], in_=spread[:].rearrange("c (p u e) -> c u p e", u=2, e=2))
+
+        def new_bank(name, tag):
+            return psum.tile([P, BANK], F32, name=name, tag=tag)
 
         prior_t, prior_grouped, prior_codes, prior_mx_scales = {}, {}, {}, {}
 
-        def transpose_prior(q):
-            prior_t[q] = psum.tile([P, 2, 2, P], F32, name="prior_t%d" % q, tag="h" if q == 1 else "tr", bufs=2)
-            words = prior_in[q][:].rearrange("p n k -> p (n k)").bitcast(F32)
-            for i in range(2):
-                for u in range(2):
-                    nc.tensor.transpose(prior_t[q][:, i, u, :], words[:, 256 * i + u : 256 * (i + 1) : 2], ident[:])
+        def transpose_prior(n, bank):
+            prior_t[n] = bank[:, 0:256].rearrange("p (u r) -> p u r", u=2)
+            words = prior_in[n].bitcast(F32)
+            for u in range(2):
+                nc.tensor.transpose(prior_t[n][:, u, :], words[:, u : 256 : 2], ident[:])
 
-        def copy_prior(q):
-            prior_grouped[q] = work.tile([P, 2 * P * 4], BF16, name="prior_grouped%d" % q, tag="prior_grouped", bufs=2, align_bytes=64)
-            for i in range(2):
-                nc.scalar.activation(
-                    out=prior_grouped[q][:, 512 * i : 512 * (i + 1)].rearrange("p (r u e) -> p r u e", u=2, e=2),
-                    in_=prior_t[q][:, i, :, :].rearrange("p u r -> p (u r)").bitcast(BF16).rearrange("p (u r e) -> p r u e", u=2, e=2),
-                    func=ACT.Copy,
-                    scale=2.0,
-                )
+        def copy_prior(n):
+            prior_grouped[n] = work.tile([P, P * 4], BF16, name="prior_grouped%d" % n, tag="prior_grouped", bufs=2, align_bytes=64)
+            nc.scalar.activation(
+                out=prior_grouped[n][:].rearrange("p (r u e) -> p r u e", u=2, e=2),
+                in_=prior_t[n].rearrange("p u r -> p (u r)").bitcast(BF16).rearrange("p (u r e) -> p r u e", u=2, e=2),
+                func=ACT.Copy,
+                scale=2.0,
+            )
 
-        def quantize_prior(q):
-            prior_codes[q] = keep.tile([P, 2 * P], U32, name="prior_codes%d" % q, align_bytes=64)
-            prior_mx_scales[q] = keep.tile([P, 2 * P], U8, name="prior_mx_scales%d" % q, align_bytes=64)
-            nc.vector.quantize_mx(out=prior_codes[q][:].bitcast(FP8X4), scales=prior_mx_scales[q][:], in_=prior_grouped[q][:])
+        def quantize_prior(n):
+            prior_codes[n] = keep.tile([P, P], U32, name="prior_codes%d" % n, align_bytes=64)
+            prior_mx_scales[n] = keep.tile([P, P], U8, name="prior_mx_scales%d" % n, align_bytes=64)
+            nc.vector.quantize_mx(out=prior_codes[n][:].bitcast(FP8X4), scales=prior_mx_scales[n][:], in_=prior_grouped[n][:])
 
-        x_scaled, x_t, x_grouped, x_codes, x_mx_scales = {}, {}, {}, {}, {}
+        x_wide, x_sorted, x_t, x_grouped, x_codes, x_mx_scales = {}, {}, {}, {}, {}, {}
 
-        def scale_x(n):
-            x_scaled[n] = work.tile([P, D], BF16, name="x_scaled%d" % n, tag="x_scaled", bufs=3)
-            for c0, c1 in ((0, 256), (256, 512), (512, 1024)) if n == 0 else ((0, 1024),):
-                nc.vector.tensor_tensor(
-                    out=x_scaled[n][:, c0:c1], in0=x_fp8[n // 2][:, n % 2, c0:c1].bitcast(FP8), in1=s_all[:, c0:c1], op=ALU.mult
-                )
+        def widen_x(n):
+            x_wide[n] = work.tile([P, D], BF16, name="x_wide%d" % n, tag="x_wide", bufs=3)
+            nc.scalar.copy(out=x_wide[n][:], in_=x_fp8[n])
 
-        def transpose_x(n):
-            x_t[n] = psum.tile([P, 2, 2, P], F32, name="x_t%d" % n, tag="tr", bufs=2)
-            words = x_scaled[n][:].bitcast(F32)
+        def sort_x(n):
+            x_sorted[n] = work.tile([P, 2, 2, P], F32, name="x_sorted%d" % n, tag="x_sorted", bufs=2)
+            nc.scalar.copy(out=x_sorted[n][:], in_=x_wide[n][:].bitcast(F32).rearrange("c (g p u) -> c g u p", g=2, u=2))
+
+        def transpose_x(n, tag="x"):
+            x_t[n] = psum.tile([P, 2, 2, P], F32, name="x_t%d" % n, tag=tag)
+            words = x_wide[n][:].bitcast(F32)
             for g in range(2):
                 for u in range(2):
-                    nc.tensor.transpose(x_t[n][:, g, u, :], words[:, 256 * g + u : 256 * (g + 1) : 2], ident[:])
+                    cols = x_sorted[n][:, g, u, :] if n in x_sorted else words[:, 256 * g + u : 256 * (g + 1) : 2]
+                    nc.tensor.transpose(x_t[n][:, u, g, :], cols, ident[:])
 
-        def copy_x(n):
-            x_grouped[n] = work.tile([P, 2 * P * 4], BF16, name="x_grouped%d" % n, tag="x_grouped", bufs=3, align_bytes=64)
-            nc.scalar.copy(
-                out=x_grouped[n][:].bitcast(F32).rearrange("p (g r u) -> p g r u", g=2, u=2),
-                in_=x_t[n][:].rearrange("p g u r -> p g r u"),
+        def new_x_tiles(n):
+            x_grouped[n] = work.tile([P, 2 * P * 4], BF16, name="x_grouped%d" % n, tag="x_grouped", bufs=2, align_bytes=64)
+            x_codes[n] = keep.tile([P, 2 * P], U32, name="x_codes%d" % n, align_bytes=64)
+            x_mx_scales[n] = keep.tile([P, 2 * P], U8, name="x_mx_scales%d" % n, align_bytes=64)
+
+        def scale_x(n):
+            new_x_tiles(n)
+            nc.vector.tensor_tensor(
+                out=x_grouped[n][:].rearrange("p (g r u e) -> p g r u e", g=2, u=2, e=2),
+                in0=x_t[n][:].rearrange("p u g r -> p (u g r)").bitcast(BF16).rearrange("p (u g r e) -> p g r u e", u=2, g=2, e=2),
+                in1=s_twice[:].rearrange("p g (u e) -> p g u e", u=2).unsqueeze(2).to_broadcast([P, 2, P, 2, 2]),
+                op=ALU.mult,
             )
 
         def quantize_x(n):
-            x_codes[n] = keep.tile([P, 2 * P], U32, name="x_codes%d" % n, align_bytes=64)
-            x_mx_scales[n] = keep.tile([P, 2 * P], U8, name="x_mx_scales%d" % n, align_bytes=64)
             nc.vector.quantize_mx(out=x_codes[n][:].bitcast(FP8X4), scales=x_mx_scales[n][:], in_=x_grouped[n][:])
+
+        first_wide, first_t = {}, {}
+
+        def widen_first(g):
+            first_wide[g] = keep.tile([P, 2, P, 2], BF16, name="first_wide%d" % g)
+            nc.vector.tensor_scalar(
+                out=first_wide[g][:].rearrange("c u p e -> c p u e"),
+                in0=x_fp8[0][:, 512 * g : 512 * (g + 1)].rearrange("c (p u e) -> c p u e", u=2, e=2),
+                scalar1=two[:], scalar2=None, op0=ALU.mult,
+            )
+
+        def transpose_first(g):
+            first_t[g] = psum.tile([P, 2, P], F32, name="first_t%d" % g, tag="h%d" % (g + 1))
+            words = first_wide[g][:].rearrange("c u p e -> c (u p e)").bitcast(F32)
+            for u in range(2):
+                nc.tensor.transpose(first_t[g][:, u, :], words[:, P * u : P * (u + 1)], ident[:])
+
+        def scale_first(g):
+            nc.vector.tensor_tensor(
+                out=x_grouped[0][:, 512 * g : 512 * (g + 1)].rearrange("p (r u e) -> p r u e", u=2, e=2),
+                in0=first_t[g][:].rearrange("p u r -> p (u r)").bitcast(BF16).rearrange("p (u r e) -> p r u e", u=2, e=2),
+                in1=s_col[:, g, :].rearrange("p (u e) -> p u e", u=2).unsqueeze(1).to_broadcast([P, P, 2, 2]),
+                op=ALU.mult,
+            )
+
+        def quantize_first(g):
+            nc.vector.quantize_mx(
+                out=x_codes[0][:, P * g : P * (g + 1)].bitcast(FP8X4), scales=x_mx_scales[0][:, P * g : P * (g + 1)],
+                in_=x_grouped[0][:, 512 * g : 512 * (g + 1)],
+            )
 
         acc_a, r_rows, r_t, r_grouped, r_codes, r_mx_scales = {}, {}, {}, {}, {}, {}
 
         def matmul_a(n):
-            acc_a[n] = psum.tile([P, G], F32, name="acc_a%d" % n, tag="a", bufs=1)
-            c0 = P * (n % 2)
-            for i in range(3):
-                if i == 0:
-                    codes, scales, w = prior_codes[n // 2][:, c0 : c0 + P], prior_mx_scales[n // 2][:, c0 : c0 + P], wp[:, 0, :]
-                else:
-                    codes, scales, w = x_codes[n][:, P * (i - 1) : P * i], x_mx_scales[n][:, P * (i - 1) : P * i], wx[:, i - 1, :]
+            acc_a[n] = psum.tile([P, G], F32, name="acc_a%d" % n, tag="a")
+            passes = [(x_codes[n][:, P * g : P * (g + 1)], x_mx_scales[n][:, P * g : P * (g + 1)], wx[:, g, :], a_scales[:, 1 + g, :]) for g in range(2)]
+            passes.append((prior_codes[n][:], prior_mx_scales[n][:], wp[:, 0, :], a_scales[:, 0, :]))
+            for i, (codes, scales, w, w_scales) in enumerate(passes):
                 nc.tensor.matmul_mx(
                     out=acc_a[n][:], lhsT=codes.bitcast(FP8X4), lhsT_scale=scales, rhs=w.bitcast(FP4X4),
-                    rhs_scale=a_scales[:, i, :], start=(i == 0), stop=(i == 2),
+                    rhs_scale=w_scales, start=(i == 0), stop=(i == 2),
                 )
 
         def add_bias(n):
@@ -191,8 +223,8 @@ def tile_pepnetpriorgatedhiddenlayer_w4_kernel(
                 out=r_rows[n][:], in0=acc_a[n][:].rearrange("c (p u e) -> c u p e", u=2, e=2), in1=bias[:], op=ALU.add
             )
 
-        def transpose_r(n):
-            r_t[n] = psum.tile([P, 2 * P], F32, name="r_t%d" % n, tag="r", bufs=1)
+        def transpose_r(n, bank):
+            r_t[n] = bank[:, 256:512]
             words = r_rows[n][:].rearrange("c u p e -> c (u p e)").bitcast(F32)
             for u in range(2):
                 nc.tensor.transpose(r_t[n][:, P * u : P * (u + 1)], words[:, P * u : P * (u + 1)], ident[:])
@@ -201,7 +233,7 @@ def tile_pepnetpriorgatedhiddenlayer_w4_kernel(
             r_grouped[n] = work.tile([P, P * 4], BF16, name="r_grouped%d" % n, tag="r_grouped", bufs=2, align_bytes=64)
             nc.scalar.activation(
                 out=r_grouped[n][:].rearrange("p (c u e) -> p c u e", u=2, e=2),
-                in_=r_t[n][:].bitcast(BF16).rearrange("p (u c e) -> p c u e", u=2, e=2),
+                in_=r_t[n].bitcast(BF16).rearrange("p (u c e) -> p c u e", u=2, e=2),
                 func=ACT.Relu,
             )
 
@@ -210,97 +242,129 @@ def tile_pepnetpriorgatedhiddenlayer_w4_kernel(
             r_mx_scales[n] = work.tile([P, P], U8, name="r_mx_scales%d" % n, tag="r_mx_scales", bufs=3, align_bytes=64)
             nc.vector.quantize_mx(out=r_codes[n][:].bitcast(FP8X4), scales=r_mx_scales[n][:], in_=r_grouped[n][:])
 
-        acc_t, acc_h, gate, res = {}, {}, {}, {}
+        acc_t, acc_h, gate = {}, {}, {}
 
-        def matmul_t(n, j):
-            acc_t[n, j] = psum.tile([P, BANK], F32, name="acc_t%d_%d" % (n, j), tag="t", bufs=2)
+        def matmul_t(n, j, tag=None):
+            acc_t[n, j] = new_bank("acc_t%d_%d" % (n, j), tag or "t%d" % j)
             nc.tensor.matmul_mx(
                 out=acc_t[n, j][:], lhsT=r_codes[n][:].bitcast(FP8X4), lhsT_scale=r_mx_scales[n][:],
-                rhs=w2[:, 0, 2 * BANK * j : 2 * BANK * (j + 1)].bitcast(FP4X4), rhs_scale=w2_sc[:, BANK * j : BANK * (j + 1)],
+                rhs=w2[:, 0, 2 * BANK * j : 2 * BANK * (j + 1)].bitcast(FP4X4), rhs_scale=w2_sc[:, 0, BANK * j : BANK * (j + 1)],
                 start=True, stop=True,
             )
 
         def sigmoid_t(n, j):
-            gate[n, j] = work.tile([P, BANK], F32, name="gate%d_%d" % (n, j), tag="gate", bufs=6)
+            gate[n, j] = work.tile([P, BANK], F32, name="gate%d_%d" % (n, j), tag="gate", bufs=4)
             nc.scalar.activation(out=gate[n, j][:], in_=acc_t[n, j][:], func=ACT.Sigmoid, scale=0.5)
 
-        def matmul_h(n, j):
-            acc_h[n, j] = psum.tile([P, BANK], F32, name="acc_h%d_%d" % (n, j), tag="h", bufs=2)
+        def matmul_h(n, j, tag=None):
+            acc_h[n, j] = new_bank("acc_h%d_%d" % (n, j), tag or "h%d" % ((2 * n + j) % 3))
             for g in range(2):
                 nc.tensor.matmul_mx(
                     out=acc_h[n, j][:], lhsT=x_codes[n][:, P * g : P * (g + 1)].bitcast(FP8X4), lhsT_scale=x_mx_scales[n][:, P * g : P * (g + 1)],
-                    rhs=wl[:, g, 2 * BANK * j : 2 * BANK * (j + 1)].bitcast(FP4X4), rhs_scale=wl_sc[:, g, BANK * j : BANK * (j + 1)],
+                    rhs=wl[j][:, g, :].bitcast(FP4X4), rhs_scale=wl_sc[:, g, BANK * j : BANK * (j + 1)],
                     start=(g == 0), stop=(g == 1),
                 )
 
         def gate_and_store(n, j):
-            if j == 0:
-                res[n] = work.tile([P, HID], F32, name="res%d" % n, tag="res", bufs=3)
-            nc.vector.scalar_tensor_tensor(
-                out=res[n][:, BANK * j : BANK * (j + 1)], in0=acc_h[n, j][:], scalar=0.0, in1=gate[n, j][:], op0=ALU.max, op1=ALU.mult
-            )
-            if n == NT - 1:
-                nc.sync.dma_start(out=out_rows[:, n, BANK * j : BANK * (j + 1)], in_=res[n][:, BANK * j : BANK * (j + 1)])
-            elif j == 1:
-                nc.sync.dma_start(out=out_rows[:, n, :], in_=res[n][:])
+            res = work.tile([P, BANK], F32, name="res%d_%d" % (n, j), tag="res", bufs=6)
+            nc.vector.scalar_tensor_tensor(out=res[:], in0=acc_h[n, j][:], scalar=0.0, in1=gate[n, j][:], op0=ALU.max, op1=ALU.mult)
+            nc.sync.dma_start(out=out_rows[:, n, BANK * j : BANK * (j + 1)], in_=res[:])
 
         def keep_tensor_busy(count):
             for i in range(count):
-                junk = psum.tile([P, BANK], F32, name="junk", tag="t", bufs=2)
-                nc.tensor.matmul(junk[:], warm[:, 0:P], warm[:], start=True, stop=True)
+                junk = new_bank("junk", "a")
+                nc.tensor.matmul(junk[:], twos[:, 0:P], twos[:], start=True, stop=True)
 
         def both_halves(stage, n):
             for j in range(2):
                 stage(n, j)
 
-        ctx.enter_context(tc.manual_schedule())
-        keep_tensor_busy(3)
-        spread_scales()
-        transpose_prior(0)
+        keep_tensor_busy(4)
+        for g in range(2):
+            widen_first(g)
+            transpose_first(g)
+        double_scales()
+        widen_x(1)
+        transpose_prior(0, new_bank("prior_bank0", "r"))
         copy_prior(0)
-        keep_tensor_busy(3)
-        scale_x(0)
-        transpose_x(0)
-        copy_x(0)
-        scale_x(1)
-        quantize_prior(0)
-        transpose_prior(1)
+        keep_tensor_busy(1)
         transpose_x(1)
-        copy_x(1)
-        quantize_x(0)
-        spread_bias()
+        transpose_prior(1, new_bank("prior_bank1", "t1"))
+        spread = spread_bias()
         copy_prior(1)
+        widen_x(2)
+        copy_bias(spread)
+        keep_tensor_busy(1)
+        new_x_tiles(0)
+        for g in range(2):
+            scale_first(g)
+        quantize_first(0)
+        quantize_prior(0)
+        quantize_first(1)
+        scale_x(1)
         matmul_a(0)
-        scale_x(2)
+        widen_x(3)
+        transpose_x(2)
+        matmul_h(0, 0)
+        quantize_prior(1)
         add_bias(0)
         quantize_x(1)
-        scale_x(3)
-        for i in range(NT + 1):
-            if i + 2 < NT:
-                transpose_x(i + 2)
-                copy_x(i + 2)
-            if i < NT:
-                transpose_r(i)
-                relu_r(i)
-            if i % 2 == 1 and (i + 3) // 2 < PAIRS:
-                transpose_prior((i + 3) // 2)
-                copy_prior((i + 3) // 2)
-            if i > 0:
-                both_halves(matmul_t, i - 1)
-                both_halves(sigmoid_t, i - 1)
-            if i + 1 < NT:
-                matmul_a(i + 1)
-            if i > 0:
-                both_halves(matmul_h, i - 1)
-            if i + 1 < NT:
-                add_bias(i + 1)
-            if i < NT:
-                quantize_r(i)
-            if i % 2 == 0 and (i + 2) // 2 < PAIRS:
-                quantize_prior((i + 2) // 2)
-            if i + 2 < NT:
-                quantize_x(i + 2)
+        scale_x(2)
+        for i in range(NT - 2):
+            bank = new_bank("r_bank%d" % i, "r")
+            if i == 0:
+                transpose_r(i, bank)
+                transpose_x(i + 3, "h2")
+                transpose_prior(i + 2, new_bank("prior_bank2", "t1"))
+            else:
+                if i + 3 < NT:
+                    transpose_x(i + 3)
+                transpose_prior(i + 2, bank)
+                transpose_r(i, bank)
+            relu_r(i)
+            if i == 0:
+                widen_x(4)
+            copy_prior(i + 2)
+            if i + 5 < NT:
+                widen_x(i + 5)
+            matmul_a(i + 1)
             if i > 0:
                 both_halves(gate_and_store, i - 1)
+            else:
+                quantize_x(2)
+            matmul_h(i, 1)
+            quantize_r(i)
             if i + 4 < NT:
-                scale_x(i + 4)
+                scale_x(i + 3)
+            if i > 0:
+                matmul_h(i + 1, 0)
+            add_bias(i + 1)
+            if i + 4 == NT:
+                scale_x(i + 3)
+            quantize_prior(i + 2)
+            if i + 3 < NT:
+                quantize_x(i + 3)
+            both_halves(matmul_t, i)
+            if i == 0:
+                matmul_h(i + 1, 0)
+            both_halves(sigmoid_t, i)
+        transpose_r(6, new_bank("r_bank6", "r"))
+        relu_r(6)
+        matmul_a(7)
+        matmul_h(6, 1, "x")
+        gate_and_store(5, 0)
+        matmul_h(7, 0, "h1")
+        add_bias(7)
+        quantize_r(6)
+        gate_and_store(5, 1)
+        transpose_r(7, new_bank("r_bank7", "r"))
+        relu_r(7)
+        both_halves(matmul_t, 6)
+        both_halves(sigmoid_t, 6)
+        matmul_h(7, 1, "h2")
+        quantize_r(7)
+        both_halves(gate_and_store, 6)
+        matmul_t(7, 0, "a")
+        matmul_t(7, 1, "r")
+        both_halves(sigmoid_t, 7)
+        both_halves(gate_and_store, 7)

@@ -89,15 +89,15 @@ def tile_pepnetpriorgatedhiddenlayer_w4_kernel(
         load_x(2, 3)
         load_scales(a_scales[:, 0:1, :], wp_scales)
         wp = load_words("wp", wp_words)
-        load_scales(wl_sc, wl_scales)
-        wl = [load_words("wl0", wl_words[:, :, 0 : 2 * BANK])]
-        load_x(3, 4)
-        wl.append(load_words("wl1", wl_words[:, :, 2 * BANK : 4 * BANK]))
         load_prior(2, 4)
+        load_x(3, 4)
         load_scales(w2_sc, w2_scales)
         w2 = load_words("w2", w2_words)
-        load_x(4, 6)
         load_prior(4, 6)
+        load_x(4, 6)
+        load_scales(wl_sc, wl_scales)
+        wl = [load_words("wl0", wl_words[:, :, 0 : 2 * BANK])]
+        wl.append(load_words("wl1", wl_words[:, :, 2 * BANK : 4 * BANK]))
         load_x(6, 8)
         load_prior(6, 8)
 
@@ -118,6 +118,13 @@ def tile_pepnetpriorgatedhiddenlayer_w4_kernel(
         def new_bank(name, tag):
             return psum.tile([P, BANK], F32, name=name, tag=tag)
 
+        joint = {}
+
+        def joint_tile(n):
+            if n not in joint:
+                joint[n] = work.tile([P, 2 * P * 4], BF16, name="joint%d" % n, tag="joint", bufs=3, align_bytes=64)
+            return joint[n]
+
         prior_t, prior_grouped, prior_codes, prior_mx_scales = {}, {}, {}, {}
 
         def transpose_prior(n, bank):
@@ -127,9 +134,12 @@ def tile_pepnetpriorgatedhiddenlayer_w4_kernel(
                 nc.tensor.transpose(prior_t[n][:, u, :], words[:, u : 256 : 2], ident[:])
 
         def copy_prior(n):
-            prior_grouped[n] = work.tile([P, P * 4], BF16, name="prior_grouped%d" % n, tag="prior_grouped", bufs=2, align_bytes=64)
+            if n < 2:
+                prior_grouped[n] = work.tile([P, P * 4], BF16, name="prior_grouped%d" % n, tag="prior_grouped", bufs=2, align_bytes=64)[:]
+            else:
+                prior_grouped[n] = joint_tile(n - 2)[:, 512:1024]
             nc.scalar.activation(
-                out=prior_grouped[n][:].rearrange("p (r u e) -> p r u e", u=2, e=2),
+                out=prior_grouped[n].rearrange("p (r u e) -> p r u e", u=2, e=2),
                 in_=prior_t[n].rearrange("p u r -> p (u r)").bitcast(BF16).rearrange("p (u r e) -> p r u e", u=2, e=2),
                 func=ACT.Copy,
                 scale=2.0,
@@ -138,24 +148,20 @@ def tile_pepnetpriorgatedhiddenlayer_w4_kernel(
         def quantize_prior(n):
             prior_codes[n] = keep.tile([P, P], U32, name="prior_codes%d" % n, align_bytes=64)
             prior_mx_scales[n] = keep.tile([P, P], U8, name="prior_mx_scales%d" % n, align_bytes=64)
-            nc.vector.quantize_mx(out=prior_codes[n][:].bitcast(FP8X4), scales=prior_mx_scales[n][:], in_=prior_grouped[n][:])
+            nc.vector.quantize_mx(out=prior_codes[n][:].bitcast(FP8X4), scales=prior_mx_scales[n][:], in_=prior_grouped[n])
 
-        x_wide, x_sorted, x_t, x_grouped, x_codes, x_mx_scales = {}, {}, {}, {}, {}, {}
+        x_wide, x_t, x_grouped, x_codes, x_mx_scales = {}, {}, {}, {}, {}
 
         def widen_x(n):
             x_wide[n] = work.tile([P, D], BF16, name="x_wide%d" % n, tag="x_wide", bufs=3)
             nc.scalar.copy(out=x_wide[n][:], in_=x_fp8[n])
-
-        def sort_x(n):
-            x_sorted[n] = work.tile([P, 2, 2, P], F32, name="x_sorted%d" % n, tag="x_sorted", bufs=2)
-            nc.scalar.copy(out=x_sorted[n][:], in_=x_wide[n][:].bitcast(F32).rearrange("c (g p u) -> c g u p", g=2, u=2))
 
         def transpose_x(n, tag="x"):
             x_t[n] = psum.tile([P, 2, 2, P], F32, name="x_t%d" % n, tag=tag)
             words = x_wide[n][:].bitcast(F32)
             for g in range(2):
                 for u in range(2):
-                    cols = x_sorted[n][:, g, u, :] if n in x_sorted else words[:, 256 * g + u : 256 * (g + 1) : 2]
+                    cols = words[:, 256 * g + u : 256 * (g + 1) : 2]
                     nc.tensor.transpose(x_t[n][:, u, g, :], cols, ident[:])
 
         def new_x_tiles(n):
@@ -205,7 +211,7 @@ def tile_pepnetpriorgatedhiddenlayer_w4_kernel(
                 in_=x_grouped[0][:, 512 * g : 512 * (g + 1)],
             )
 
-        acc_a, r_rows, r_t, r_grouped, r_codes, r_mx_scales = {}, {}, {}, {}, {}, {}
+        acc_a, r_rows, r_t, r_codes, r_mx_scales = {}, {}, {}, {}, {}
 
         def matmul_a(n):
             acc_a[n] = psum.tile([P, G], F32, name="acc_a%d" % n, tag="a")
@@ -230,17 +236,20 @@ def tile_pepnetpriorgatedhiddenlayer_w4_kernel(
                 nc.tensor.transpose(r_t[n][:, P * u : P * (u + 1)], words[:, P * u : P * (u + 1)], ident[:])
 
         def relu_r(n):
-            r_grouped[n] = work.tile([P, P * 4], BF16, name="r_grouped%d" % n, tag="r_grouped", bufs=2, align_bytes=64)
             nc.scalar.activation(
-                out=r_grouped[n][:].rearrange("p (c u e) -> p c u e", u=2, e=2),
+                out=joint_tile(n)[:, 0:512].rearrange("p (c u e) -> p c u e", u=2, e=2),
                 in_=r_t[n].bitcast(BF16).rearrange("p (u c e) -> p c u e", u=2, e=2),
                 func=ACT.Relu,
             )
 
         def quantize_r(n):
-            r_codes[n] = work.tile([P, P], U32, name="r_codes%d" % n, tag="r_codes", bufs=3, align_bytes=64)
-            r_mx_scales[n] = work.tile([P, P], U8, name="r_mx_scales%d" % n, tag="r_mx_scales", bufs=3, align_bytes=64)
-            nc.vector.quantize_mx(out=r_codes[n][:].bitcast(FP8X4), scales=r_mx_scales[n][:], in_=r_grouped[n][:])
+            width = 2 * P if n + 2 < NT else P
+            codes = keep.tile([P, width], U32, name="r_codes%d" % n, align_bytes=64)
+            scales = keep.tile([P, width], U8, name="r_mx_scales%d" % n, align_bytes=64)
+            nc.vector.quantize_mx(out=codes[:].bitcast(FP8X4), scales=scales[:], in_=joint[n][:, 0 : 4 * width])
+            r_codes[n], r_mx_scales[n] = codes[:, 0:P], scales[:, 0:P]
+            if n + 2 < NT:
+                prior_codes[n + 2], prior_mx_scales[n + 2] = codes[:, P : 2 * P], scales[:, P : 2 * P]
 
         acc_t, acc_h, gate = {}, {}, {}
 
@@ -291,9 +300,10 @@ def tile_pepnetpriorgatedhiddenlayer_w4_kernel(
         transpose_x(1)
         transpose_prior(1, new_bank("prior_bank1", "t1"))
         spread = spread_bias()
-        copy_prior(1)
         widen_x(2)
+        copy_prior(1)
         copy_bias(spread)
+        widen_x(3)
         keep_tensor_busy(1)
         new_x_tiles(0)
         for g in range(2):
@@ -303,68 +313,45 @@ def tile_pepnetpriorgatedhiddenlayer_w4_kernel(
         quantize_first(1)
         scale_x(1)
         matmul_a(0)
-        widen_x(3)
-        transpose_x(2)
-        matmul_h(0, 0)
-        quantize_prior(1)
         add_bias(0)
         quantize_x(1)
-        scale_x(2)
-        for i in range(NT - 2):
-            bank = new_bank("r_bank%d" % i, "r")
-            if i == 0:
-                transpose_r(i, bank)
-                transpose_x(i + 3, "h2")
-                transpose_prior(i + 2, new_bank("prior_bank2", "t1"))
-            else:
+        quantize_prior(1)
+        for i in range(NT + 1):
+            if i + 2 < NT:
+                transpose_x(i + 2, "x" if i > 0 else "h0")
+            if i < NT:
+                bank = new_bank("r_bank%d" % i, "r")
+                if i == 0:
+                    transpose_prior(2, new_bank("prior_bank2", "t1"))
                 if i + 3 < NT:
-                    transpose_x(i + 3)
-                transpose_prior(i + 2, bank)
+                    transpose_prior(i + 3, bank)
                 transpose_r(i, bank)
-            relu_r(i)
             if i == 0:
-                widen_x(4)
-            copy_prior(i + 2)
-            if i + 5 < NT:
-                widen_x(i + 5)
-            matmul_a(i + 1)
+                copy_prior(2)
+            if 0 < i and i + 3 < NT:
+                widen_x(i + 3)
+            if i < NT:
+                relu_r(i)
+            if i + 3 < NT:
+                copy_prior(i + 3)
+            if 0 < i < NT:
+                both_halves(matmul_t, i - 1)
+            if i == NT:
+                matmul_t(i - 1, 0, "a")
+                matmul_t(i - 1, 1, "x")
+            if i > 0:
+                both_halves(sigmoid_t, i - 1)
+            if i + 1 < NT:
+                matmul_a(i + 1)
+            if i > 0:
+                both_halves(matmul_h, i - 1)
+            if i + 2 < NT:
+                scale_x(i + 2)
+            if i + 1 < NT:
+                add_bias(i + 1)
+            if i < NT:
+                quantize_r(i)
+            if i + 2 < NT:
+                quantize_x(i + 2)
             if i > 0:
                 both_halves(gate_and_store, i - 1)
-            else:
-                quantize_x(2)
-            matmul_h(i, 1)
-            quantize_r(i)
-            if i + 4 < NT:
-                scale_x(i + 3)
-            if i > 0:
-                matmul_h(i + 1, 0)
-            add_bias(i + 1)
-            if i + 4 == NT:
-                scale_x(i + 3)
-            quantize_prior(i + 2)
-            if i + 3 < NT:
-                quantize_x(i + 3)
-            both_halves(matmul_t, i)
-            if i == 0:
-                matmul_h(i + 1, 0)
-            both_halves(sigmoid_t, i)
-        transpose_r(6, new_bank("r_bank6", "r"))
-        relu_r(6)
-        matmul_a(7)
-        matmul_h(6, 1, "x")
-        gate_and_store(5, 0)
-        matmul_h(7, 0, "h1")
-        add_bias(7)
-        quantize_r(6)
-        gate_and_store(5, 1)
-        transpose_r(7, new_bank("r_bank7", "r"))
-        relu_r(7)
-        both_halves(matmul_t, 6)
-        both_halves(sigmoid_t, 6)
-        matmul_h(7, 1, "h2")
-        quantize_r(7)
-        both_halves(gate_and_store, 6)
-        matmul_t(7, 0, "a")
-        matmul_t(7, 1, "r")
-        both_halves(sigmoid_t, 7)
-        both_halves(gate_and_store, 7)

@@ -6,6 +6,7 @@ from concourse.masks import make_identity
 P = 128
 TOKENS, D, PRIOR, G, HID = 1024, 1024, 512, 512, 1024
 NT = TOKENS // P
+LATE = 5
 BANK = 512
 FLOPS = 2 * TOKENS * (D * G + PRIOR * G + G * HID + D * HID)
 
@@ -46,8 +47,6 @@ def tile_pepnetpriorgatedhiddenlayer_w4_kernel(
         wl_sc = keep.tile([P, 2, HID], U8, name="wl_sc", align_bytes=64)
         nc.vector.memset(a_scales[:].rearrange("p c n -> p (c n)").bitcast(I32), 0)
         nc.vector.memset(b_row[:], 0.0)
-        for plane in (wl_sc, w2_sc):
-            nc.vector.memset(plane[:].rearrange("p c n -> p (c n)").bitcast(I32), 0)
 
         x_rows = x_bytes.rearrange("(p n) k -> p n k", n=NT)
         prior_rows = prior.rearrange("(p n) k -> p n k", n=NT)
@@ -85,21 +84,12 @@ def tile_pepnetpriorgatedhiddenlayer_w4_kernel(
         load_prior(0, 2)
         load_scales(a_scales[:, 1:3, :], wx_scales)
         wx = load_words("wx", wx_words)
-        nc.sync.dma_start(out=b_row[0:1, :], in_=b1.rearrange("(o n) -> o n", o=1))
         load_x(2, 3)
+        nc.sync.dma_start(out=b_row[0:1, :], in_=b1.rearrange("(o n) -> o n", o=1))
         load_scales(a_scales[:, 0:1, :], wp_scales)
         wp = load_words("wp", wp_words)
         load_prior(2, 4)
         load_x(3, 4)
-        load_scales(w2_sc, w2_scales)
-        w2 = load_words("w2", w2_words)
-        load_prior(4, 6)
-        load_x(4, 6)
-        load_scales(wl_sc, wl_scales)
-        wl = [load_words("wl0", wl_words[:, :, 0 : 2 * BANK])]
-        wl.append(load_words("wl1", wl_words[:, :, 2 * BANK : 4 * BANK]))
-        load_x(6, 8)
-        load_prior(6, 8)
 
         s_twice = keep.tile([P, 2, 4], F32, name="s_twice")
         bias = keep.tile([P, 2, P, 2], F32, name="bias")
@@ -150,22 +140,31 @@ def tile_pepnetpriorgatedhiddenlayer_w4_kernel(
             prior_mx_scales[n] = keep.tile([P, P], U8, name="prior_mx_scales%d" % n, align_bytes=64)
             nc.vector.quantize_mx(out=prior_codes[n][:].bitcast(FP8X4), scales=prior_mx_scales[n][:], in_=prior_grouped[n])
 
-        x_wide, x_t, x_grouped, x_codes, x_mx_scales = {}, {}, {}, {}, {}
+        x_wide, x_sorted, x_t, x_grouped, x_codes, x_mx_scales = {}, {}, {}, {}, {}, {}
 
         def widen_x(n):
-            x_wide[n] = work.tile([P, D], BF16, name="x_wide%d" % n, tag="x_wide", bufs=3)
-            nc.scalar.copy(out=x_wide[n][:], in_=x_fp8[n])
+            if n < LATE:
+                x_wide[n] = work.tile([P, D], BF16, name="x_wide%d" % n, tag="x_wide", bufs=3)
+                nc.scalar.copy(out=x_wide[n][:], in_=x_fp8[n])
+            else:
+                x_wide[n] = work.tile([P, D], BF16, name="x_wide%d" % n, tag="x_late%d" % n, bufs=1, align_bytes=64)
+                nc.gpsimd.tensor_copy(out=x_wide[n][:], in_=x_fp8[n])
+
+        def sort_x(n):
+            x_sorted[n] = work.tile([P, 2, 2, P], F32, name="x_sorted%d" % n, tag="x_sorted", bufs=2)
+            nc.scalar.copy(out=x_sorted[n][:], in_=x_wide[n][:].bitcast(F32).rearrange("c (g p u) -> c g u p", g=2, u=2))
 
         def transpose_x(n, tag="x"):
             x_t[n] = psum.tile([P, 2, 2, P], F32, name="x_t%d" % n, tag=tag)
             words = x_wide[n][:].bitcast(F32)
             for g in range(2):
                 for u in range(2):
-                    cols = words[:, 256 * g + u : 256 * (g + 1) : 2]
+                    cols = x_sorted[n][:, g, u, :] if n in x_sorted else words[:, 256 * g + u : 256 * (g + 1) : 2]
                     nc.tensor.transpose(x_t[n][:, u, g, :], cols, ident[:])
 
         def new_x_tiles(n):
-            x_grouped[n] = work.tile([P, 2 * P * 4], BF16, name="x_grouped%d" % n, tag="x_grouped", bufs=2, align_bytes=64)
+            tag = "x_late%d" % (n + 3) if LATE <= n + 3 < NT else "x_grouped"
+            x_grouped[n] = work.tile([P, 2 * P * 4], BF16, name="x_grouped%d" % n, tag=tag, bufs=1 if LATE <= n + 3 < NT else 2, align_bytes=64)
             x_codes[n] = keep.tile([P, 2 * P], U32, name="x_codes%d" % n, align_bytes=64)
             x_mx_scales[n] = keep.tile([P, 2 * P], U8, name="x_mx_scales%d" % n, align_bytes=64)
 
@@ -274,14 +273,16 @@ def tile_pepnetpriorgatedhiddenlayer_w4_kernel(
                     start=(g == 0), stop=(g == 1),
                 )
 
-        def gate_and_store(n, j):
-            res = work.tile([P, BANK], F32, name="res%d_%d" % (n, j), tag="res", bufs=6)
-            nc.vector.scalar_tensor_tensor(out=res[:], in0=acc_h[n, j][:], scalar=0.0, in1=gate[n, j][:], op0=ALU.max, op1=ALU.mult)
-            nc.sync.dma_start(out=out_rows[:, n, BANK * j : BANK * (j + 1)], in_=res[:])
+        def gate_and_store(n, j, c0=0, c1=BANK):
+            res = work.tile([P, c1 - c0], F32, name="res%d_%d_%d" % (n, j, c0), tag="res", bufs=6)
+            nc.vector.scalar_tensor_tensor(
+                out=res[:], in0=acc_h[n, j][:, c0:c1], scalar=0.0, in1=gate[n, j][:, c0:c1], op0=ALU.max, op1=ALU.mult
+            )
+            nc.sync.dma_start(out=out_rows[:, n, BANK * j + c0 : BANK * j + c1], in_=res[:])
 
-        def keep_tensor_busy(count):
+        def keep_tensor_busy(count, tag="a"):
             for i in range(count):
-                junk = new_bank("junk", "a")
+                junk = new_bank("junk", tag)
                 nc.tensor.matmul(junk[:], twos[:, 0:P], twos[:], start=True, stop=True)
 
         def both_halves(stage, n):
@@ -293,18 +294,28 @@ def tile_pepnetpriorgatedhiddenlayer_w4_kernel(
             widen_first(g)
             transpose_first(g)
         double_scales()
+        for plane in (w2_sc, wl_sc):
+            nc.vector.memset(plane[:].rearrange("p c n -> p (c n)").bitcast(I32), 0)
+        load_scales(w2_sc, w2_scales)
+        w2 = load_words("w2", w2_words)
+        load_prior(4, 6)
+        load_x(4, 6)
+        load_scales(wl_sc, wl_scales)
+        wl = [load_words("wl0", wl_words[:, :, 0 : 2 * BANK])]
+        wl.append(load_words("wl1", wl_words[:, :, 2 * BANK : 4 * BANK]))
+        load_x(6, 8)
+        load_prior(6, 8)
         widen_x(1)
         transpose_prior(0, new_bank("prior_bank0", "r"))
         copy_prior(0)
         keep_tensor_busy(1)
         transpose_x(1)
-        transpose_prior(1, new_bank("prior_bank1", "t1"))
         spread = spread_bias()
+        transpose_prior(1, new_bank("prior_bank1", "t1"))
         widen_x(2)
-        copy_prior(1)
         copy_bias(spread)
+        copy_prior(1)
         widen_x(3)
-        keep_tensor_busy(1)
         new_x_tiles(0)
         for g in range(2):
             scale_first(g)
@@ -325,11 +336,15 @@ def tile_pepnetpriorgatedhiddenlayer_w4_kernel(
                     transpose_prior(2, new_bank("prior_bank2", "t1"))
                 if i + 3 < NT:
                     transpose_prior(i + 3, bank)
+                if i == 0:
+                    keep_tensor_busy(1, "h1")
                 transpose_r(i, bank)
             if i == 0:
                 copy_prior(2)
-            if 0 < i and i + 3 < NT:
+            if 0 < i and i + 3 < LATE:
                 widen_x(i + 3)
+            if LATE <= i + 3 < NT:
+                sort_x(i + 3)
             if i < NT:
                 relu_r(i)
             if i + 3 < NT:
@@ -353,5 +368,11 @@ def tile_pepnetpriorgatedhiddenlayer_w4_kernel(
                 quantize_r(i)
             if i + 2 < NT:
                 quantize_x(i + 2)
+            if i + 5 < NT:
+                widen_x(i + 5)
+            if i == 4 + 1:
+                gate_and_store(i - 2, 1)
             if i > 0:
-                both_halves(gate_and_store, i - 1)
+                gate_and_store(i - 1, 0)
+            if 0 < i and i != 4:
+                gate_and_store(i - 1, 1)

@@ -7,6 +7,7 @@ P = 128
 TOKENS, D, PRIOR, G, HID = 1024, 1024, 512, 512, 1024
 NT = TOKENS // P
 LATE = 5
+SHARE = 192
 BANK = 512
 FLOPS = 2 * TOKENS * (D * G + PRIOR * G + G * HID + D * HID)
 
@@ -250,7 +251,7 @@ def tile_pepnetpriorgatedhiddenlayer_w4_kernel(
             if n + 2 < NT:
                 prior_codes[n + 2], prior_mx_scales[n + 2] = codes[:, P : 2 * P], scales[:, P : 2 * P]
 
-        acc_t, acc_h, gate = {}, {}, {}
+        acc_t, acc_h, gate, h_part, pending = {}, {}, {}, {}, {}
 
         def matmul_t(n, j, tag=None):
             acc_t[n, j] = new_bank("acc_t%d_%d" % (n, j), tag or "t%d" % j)
@@ -273,12 +274,24 @@ def tile_pepnetpriorgatedhiddenlayer_w4_kernel(
                     start=(g == 0), stop=(g == 1),
                 )
 
-        def gate_and_store(n, j, c0=0, c1=BANK):
-            res = work.tile([P, c1 - c0], F32, name="res%d_%d_%d" % (n, j, c0), tag="res", bufs=6)
+        def gate_and_store(n, j, shared=0):
+            res = work.tile([P, BANK], F32, name="res%d_%d" % (n, j), tag="res", bufs=6)
+            c0 = BANK - shared
             nc.vector.scalar_tensor_tensor(
-                out=res[:], in0=acc_h[n, j][:, c0:c1], scalar=0.0, in1=gate[n, j][:, c0:c1], op0=ALU.max, op1=ALU.mult
+                out=res[:, 0:c0], in0=acc_h[n, j][:, 0:c0], scalar=0.0, in1=gate[n, j][:, 0:c0], op0=ALU.max, op1=ALU.mult
             )
-            nc.sync.dma_start(out=out_rows[:, n, BANK * j + c0 : BANK * j + c1], in_=res[:])
+            if shared:
+                pending[n] = res
+            else:
+                nc.sync.dma_start(out=out_rows[:, n, BANK * j : BANK * (j + 1)], in_=res[:])
+
+        def relu_h(n):
+            h_part[n] = work.tile([P, SHARE], F32, name="h_part%d" % n, tag="h_part", bufs=2)
+            nc.scalar.activation(out=h_part[n][:], in_=acc_h[n, 0][:, BANK - SHARE : BANK], func=ACT.Relu)
+
+        def finish_gate(n):
+            nc.gpsimd.tensor_tensor(out=pending[n][:, BANK - SHARE : BANK], in0=h_part[n][:], in1=gate[n, 0][:, BANK - SHARE : BANK], op=ALU.mult)
+            nc.sync.dma_start(out=out_rows[:, n, 0:BANK], in_=pending[n][:])
 
         def keep_tensor_busy(count, tag="a"):
             for i in range(count):
@@ -347,6 +360,9 @@ def tile_pepnetpriorgatedhiddenlayer_w4_kernel(
                 sort_x(i + 3)
             if i < NT:
                 relu_r(i)
+            if 1 < i < 6:
+                relu_h(i - 2)
+                finish_gate(i - 2)
             if i + 3 < NT:
                 copy_prior(i + 3)
             if 0 < i < NT:
@@ -373,6 +389,6 @@ def tile_pepnetpriorgatedhiddenlayer_w4_kernel(
             if i == 4 + 1:
                 gate_and_store(i - 2, 1)
             if i > 0:
-                gate_and_store(i - 1, 0)
+                gate_and_store(i - 1, 0, SHARE if i <= 4 else 0)
             if 0 < i and i != 4:
                 gate_and_store(i - 1, 1)

@@ -6,8 +6,8 @@ from concourse.masks import make_identity
 P = 128
 TOKENS, D, PRIOR, G, HID = 1024, 1024, 512, 512, 1024
 NT = TOKENS // P
-LATE = 5
-SHARE = 192
+LATE = 6
+SHARE = 256
 BANK = 512
 FLOPS = 2 * TOKENS * (D * G + PRIOR * G + G * HID + D * HID)
 
@@ -48,6 +48,7 @@ def tile_pepnetpriorgatedhiddenlayer_w4_kernel(
         wl_sc = keep.tile([P, 2, HID], U8, name="wl_sc", align_bytes=64)
         nc.vector.memset(a_scales[:].rearrange("p c n -> p (c n)").bitcast(I32), 0)
         nc.vector.memset(b_row[:], 0.0)
+        nc.vector.memset(wl_sc[:].rearrange("p c n -> p (c n)").bitcast(I32), 0)
 
         x_rows = x_bytes.rearrange("(p n) k -> p n k", n=NT)
         prior_rows = prior.rearrange("(p n) k -> p n k", n=NT)
@@ -81,12 +82,11 @@ def tile_pepnetpriorgatedhiddenlayer_w4_kernel(
         load_x(0, 1)
         s_col = keep.tile([P, 2, 4], F32, name="s_col")
         nc.sync.dma_start(out=s_col[:], in_=x_scale.rearrange("o (g p m) -> p (o g) m", g=2, m=4))
-        load_x(1, 2)
+        load_x(1, 3)
         load_prior(0, 2)
         load_scales(a_scales[:, 1:3, :], wx_scales)
-        wx = load_words("wx", wx_words)
-        load_x(2, 3)
         nc.sync.dma_start(out=b_row[0:1, :], in_=b1.rearrange("(o n) -> o n", o=1))
+        wx = load_words("wx", wx_words)
         load_scales(a_scales[:, 0:1, :], wp_scales)
         wp = load_words("wp", wp_words)
         load_prior(2, 4)
@@ -302,13 +302,12 @@ def tile_pepnetpriorgatedhiddenlayer_w4_kernel(
             for j in range(2):
                 stage(n, j)
 
-        keep_tensor_busy(4)
+        keep_tensor_busy(3)
         for g in range(2):
             widen_first(g)
             transpose_first(g)
         double_scales()
-        for plane in (w2_sc, wl_sc):
-            nc.vector.memset(plane[:].rearrange("p c n -> p (c n)").bitcast(I32), 0)
+        nc.vector.memset(w2_sc[:].rearrange("p c n -> p (c n)").bitcast(I32), 0)
         load_scales(w2_sc, w2_scales)
         w2 = load_words("w2", w2_words)
         load_prior(4, 6)
@@ -321,12 +320,12 @@ def tile_pepnetpriorgatedhiddenlayer_w4_kernel(
         widen_x(1)
         transpose_prior(0, new_bank("prior_bank0", "r"))
         copy_prior(0)
+        spread = spread_bias()
         keep_tensor_busy(1)
         transpose_x(1)
-        spread = spread_bias()
         transpose_prior(1, new_bank("prior_bank1", "t1"))
-        widen_x(2)
         copy_bias(spread)
+        widen_x(2)
         copy_prior(1)
         widen_x(3)
         new_x_tiles(0)
@@ -341,16 +340,16 @@ def tile_pepnetpriorgatedhiddenlayer_w4_kernel(
         quantize_x(1)
         quantize_prior(1)
         for i in range(NT + 1):
-            if i + 2 < NT:
-                transpose_x(i + 2, "x" if i > 0 else "h0")
+            if 0 < i and i + 2 < NT:
+                transpose_x(i + 2)
             if i < NT:
                 bank = new_bank("r_bank%d" % i, "r")
                 if i == 0:
-                    transpose_prior(2, new_bank("prior_bank2", "t1"))
-                if i + 3 < NT:
+                    transpose_prior(2, new_bank("prior_bank2", "h1"))
+                    transpose_prior(3, new_bank("prior_bank3", "h2"))
+                    transpose_x(2, "h0")
+                elif i + 3 < NT:
                     transpose_prior(i + 3, bank)
-                if i == 0:
-                    keep_tensor_busy(1, "h1")
                 transpose_r(i, bank)
             if i == 0:
                 copy_prior(2)
@@ -360,7 +359,7 @@ def tile_pepnetpriorgatedhiddenlayer_w4_kernel(
                 sort_x(i + 3)
             if i < NT:
                 relu_r(i)
-            if 1 < i < 6:
+            if 3 < i < 6:
                 relu_h(i - 2)
                 finish_gate(i - 2)
             if i + 3 < NT:
@@ -384,11 +383,11 @@ def tile_pepnetpriorgatedhiddenlayer_w4_kernel(
                 quantize_r(i)
             if i + 2 < NT:
                 quantize_x(i + 2)
-            if i + 5 < NT:
+            if LATE <= i + 5 < NT:
                 widen_x(i + 5)
             if i == 4 + 1:
                 gate_and_store(i - 2, 1)
             if i > 0:
-                gate_and_store(i - 1, 0, SHARE if i <= 4 else 0)
+                gate_and_store(i - 1, 0, SHARE if 2 < i <= 4 else 0)
             if 0 < i and i != 4:
                 gate_and_store(i - 1, 1)

@@ -46,8 +46,8 @@ def tile_pepnetpriorgatedhiddenlayer_w4_kernel(
         a_scales = keep.tile([P, 3, G], U8, name="a_scales", align_bytes=64)
         w2_sc = keep.tile([P, 1, HID], U8, name="w2_sc", align_bytes=64)
         wl_sc = keep.tile([P, 2, HID], U8, name="wl_sc", align_bytes=64)
-        nc.vector.memset(a_scales[:].rearrange("p c n -> p (c n)").bitcast(I32), 0)
         nc.vector.memset(b_row[:], 0.0)
+        nc.vector.memset(a_scales[:].rearrange("p c n -> p (c n)").bitcast(I32), 0)
         nc.vector.memset(wl_sc[:].rearrange("p c n -> p (c n)").bitcast(I32), 0)
 
         x_rows = x_bytes.rearrange("(p n) k -> p n k", n=NT)
@@ -84,11 +84,11 @@ def tile_pepnetpriorgatedhiddenlayer_w4_kernel(
         nc.sync.dma_start(out=s_col[:], in_=x_scale.rearrange("o (g p m) -> p (o g) m", g=2, m=4))
         load_x(1, 3)
         load_prior(0, 2)
-        load_scales(a_scales[:, 1:3, :], wx_scales)
         nc.sync.dma_start(out=b_row[0:1, :], in_=b1.rearrange("(o n) -> o n", o=1))
+        load_scales(a_scales[:, 1:3, :], wx_scales)
         wx = load_words("wx", wx_words)
-        load_scales(a_scales[:, 0:1, :], wp_scales)
         wp = load_words("wp", wp_words)
+        load_scales(a_scales[:, 0:1, :], wp_scales)
         load_prior(2, 4)
         load_x(3, 4)
 
@@ -266,7 +266,7 @@ def tile_pepnetpriorgatedhiddenlayer_w4_kernel(
             nc.scalar.activation(out=gate[n, j][:], in_=acc_t[n, j][:], func=ACT.Sigmoid, scale=0.5)
 
         def matmul_h(n, j, tag=None):
-            acc_h[n, j] = new_bank("acc_h%d_%d" % (n, j), tag or "h%d" % ((2 * n + j) % 3))
+            acc_h[n, j] = new_bank("acc_h%d_%d" % (n, j), tag or "h%d" % ((2 * n + j + 2) % 3))
             for g in range(2):
                 nc.tensor.matmul_mx(
                     out=acc_h[n, j][:], lhsT=x_codes[n][:, P * g : P * (g + 1)].bitcast(FP8X4), lhsT_scale=x_mx_scales[n][:, P * g : P * (g + 1)],
@@ -308,22 +308,22 @@ def tile_pepnetpriorgatedhiddenlayer_w4_kernel(
             transpose_first(g)
         double_scales()
         nc.vector.memset(w2_sc[:].rearrange("p c n -> p (c n)").bitcast(I32), 0)
-        load_scales(w2_sc, w2_scales)
-        w2 = load_words("w2", w2_words)
-        load_prior(4, 6)
-        load_x(4, 6)
         load_scales(wl_sc, wl_scales)
         wl = [load_words("wl0", wl_words[:, :, 0 : 2 * BANK])]
+        load_prior(4, 6)
+        load_scales(w2_sc, w2_scales)
+        w2 = load_words("w2", w2_words)
+        load_x(4, 6)
         wl.append(load_words("wl1", wl_words[:, :, 2 * BANK : 4 * BANK]))
         load_x(6, 8)
         load_prior(6, 8)
         widen_x(1)
+        spread = spread_bias()
         transpose_prior(0, new_bank("prior_bank0", "r"))
         copy_prior(0)
-        spread = spread_bias()
+        transpose_prior(1, new_bank("prior_bank1", "t1"))
         keep_tensor_busy(1)
         transpose_x(1)
-        transpose_prior(1, new_bank("prior_bank1", "t1"))
         copy_bias(spread)
         widen_x(2)
         copy_prior(1)
@@ -332,8 +332,8 @@ def tile_pepnetpriorgatedhiddenlayer_w4_kernel(
         for g in range(2):
             scale_first(g)
         quantize_first(0)
-        quantize_prior(0)
         quantize_first(1)
+        quantize_prior(0)
         scale_x(1)
         matmul_a(0)
         add_bias(0)
@@ -345,8 +345,8 @@ def tile_pepnetpriorgatedhiddenlayer_w4_kernel(
             if i < NT:
                 bank = new_bank("r_bank%d" % i, "r")
                 if i == 0:
-                    transpose_prior(2, new_bank("prior_bank2", "h1"))
-                    transpose_prior(3, new_bank("prior_bank3", "h2"))
+                    transpose_prior(2, new_bank("prior_bank2", "t0"))
+                    transpose_prior(3, new_bank("prior_bank3", "h1"))
                     transpose_x(2, "h0")
                 elif i + 3 < NT:
                     transpose_prior(i + 3, bank)
@@ -373,7 +373,9 @@ def tile_pepnetpriorgatedhiddenlayer_w4_kernel(
                 both_halves(sigmoid_t, i - 1)
             if i + 1 < NT:
                 matmul_a(i + 1)
-            if i > 0:
+            if i < 2:
+                matmul_h(0, i)
+            else:
                 both_halves(matmul_h, i - 1)
             if i + 2 < NT:
                 scale_x(i + 2)

@@ -37,6 +37,7 @@ def tile_pepnetpriorgatedhiddenlayer_w4_kernel(
         nc.gpsimd.memset(two[:], 2.0)
         ident = keep.tile([P, P], F32, name="ident")
         make_identity(nc, ident[:])
+        ident_bf = keep.tile([P, P], BF16, name="ident_bf")
         twos = keep.tile([P, BANK], BF16, name="twos")
         nc.vector.memset(twos[:], 2.0)
         table_out = keep.tile([P, 1], F32, name="table_out")
@@ -229,6 +230,21 @@ def tile_pepnetpriorgatedhiddenlayer_w4_kernel(
                 out=r_rows[n][:], in0=acc_a[n][:].rearrange("c (p u e) -> c u p e", u=2, e=2), in1=bias[:], op=ALU.add
             )
 
+        def add_bias_planes(n):
+            r_rows[n] = work.tile([P, 4, P], BF16, name="r_rows%d" % n, tag="r_rows", bufs=2)
+            nc.vector.tensor_tensor(
+                out=r_rows[n][:].rearrange("c (u e) p -> c u e p", e=2), in0=acc_a[n][:].rearrange("c (p u e) -> c u e p", u=2, e=2),
+                in1=bias[:].rearrange("c u p e -> c u e p"), op=ALU.add,
+            )
+
+        def turn_r(n):
+            r_t[n] = psum.tile([P, 4, P], F32, name="r_turned%d" % n, tag="r")
+            for m in range(4):
+                nc.tensor.matmul(r_t[n][:, m, :], r_rows[n][:, m, :], ident_bf[:], start=True, stop=True)
+
+        def relu_turned(n):
+            nc.scalar.activation(out=joint_tile(n)[:, 0:512].rearrange("p (c m) -> p c m", m=4), in_=r_t[n][:].rearrange("p m c -> p c m"), func=ACT.Relu)
+
         def transpose_r(n, bank):
             r_t[n] = bank[:, 256:512]
             words = r_rows[n][:].rearrange("c u p e -> c (u p e)").bitcast(F32)
@@ -251,7 +267,7 @@ def tile_pepnetpriorgatedhiddenlayer_w4_kernel(
             if n + 2 < NT:
                 prior_codes[n + 2], prior_mx_scales[n + 2] = codes[:, P : 2 * P], scales[:, P : 2 * P]
 
-        acc_t, acc_h, gate, h_part, pending = {}, {}, {}, {}, {}
+        acc_t, acc_h, gate, result = {}, {}, {}, {}
 
         def matmul_t(n, j, tag=None):
             acc_t[n, j] = new_bank("acc_t%d_%d" % (n, j), tag or "t%d" % j)
@@ -274,24 +290,23 @@ def tile_pepnetpriorgatedhiddenlayer_w4_kernel(
                     start=(g == 0), stop=(g == 1),
                 )
 
-        def gate_and_store(n, j, shared=0):
-            res = work.tile([P, BANK], F32, name="res%d_%d" % (n, j), tag="res", bufs=6)
-            c0 = BANK - shared
+        def result_tile(n, j):
+            if (n, j) not in result:
+                result[n, j] = work.tile([P, BANK], F32, name="res%d_%d" % (n, j), tag="res", bufs=6)
+            return result[n, j]
+
+        def gate_and_store(n, j):
+            c0 = BANK - SHARE if (n, j) in result else BANK
+            res = result_tile(n, j)
             nc.vector.scalar_tensor_tensor(
                 out=res[:, 0:c0], in0=acc_h[n, j][:, 0:c0], scalar=0.0, in1=gate[n, j][:, 0:c0], op0=ALU.max, op1=ALU.mult
             )
-            if shared:
-                pending[n] = res
-            else:
-                nc.sync.dma_start(out=out_rows[:, n, BANK * j : BANK * (j + 1)], in_=res[:])
+            nc.sync.dma_start(out=out_rows[:, n, BANK * j : BANK * (j + 1)], in_=res[:])
 
-        def relu_h(n):
-            h_part[n] = work.tile([P, SHARE], F32, name="h_part%d" % n, tag="h_part", bufs=2)
-            nc.scalar.activation(out=h_part[n][:], in_=acc_h[n, 0][:, BANK - SHARE : BANK], func=ACT.Relu)
-
-        def finish_gate(n):
-            nc.gpsimd.tensor_tensor(out=pending[n][:, BANK - SHARE : BANK], in0=h_part[n][:], in1=gate[n, 0][:, BANK - SHARE : BANK], op=ALU.mult)
-            nc.sync.dma_start(out=out_rows[:, n, 0:BANK], in_=pending[n][:])
+        def share_gate(n):
+            h_part = work.tile([P, SHARE], F32, name="h_part%d" % n, tag="h_part", bufs=2)
+            nc.scalar.activation(out=h_part[:], in_=acc_h[n, 0][:, BANK - SHARE : BANK], func=ACT.Relu)
+            nc.gpsimd.tensor_tensor(out=result_tile(n, 0)[:, BANK - SHARE : BANK], in0=h_part[:], in1=gate[n, 0][:, BANK - SHARE : BANK], op=ALU.mult)
 
         def keep_tensor_busy(count, tag="a"):
             for i in range(count):
@@ -317,6 +332,7 @@ def tile_pepnetpriorgatedhiddenlayer_w4_kernel(
         wl.append(load_words("wl1", wl_words[:, :, 2 * BANK : 4 * BANK]))
         load_x(6, 8)
         load_prior(6, 8)
+        nc.scalar.copy(out=ident_bf[:], in_=ident[:])
         widen_x(1)
         spread = spread_bias()
         transpose_prior(0, new_bank("prior_bank0", "r"))
@@ -339,57 +355,80 @@ def tile_pepnetpriorgatedhiddenlayer_w4_kernel(
         add_bias(0)
         quantize_x(1)
         quantize_prior(1)
-        for i in range(NT + 1):
-            if 0 < i and i + 2 < NT:
+        for i in range(NT - 3):
+            if i > 0:
                 transpose_x(i + 2)
-            if i < NT:
-                bank = new_bank("r_bank%d" % i, "r")
-                if i == 0:
-                    transpose_prior(2, new_bank("prior_bank2", "t0"))
-                    transpose_prior(3, new_bank("prior_bank3", "h1"))
-                    transpose_x(2, "h0")
-                elif i + 3 < NT:
-                    transpose_prior(i + 3, bank)
-                transpose_r(i, bank)
+            bank = new_bank("r_bank%d" % i, "r")
+            if i == 0:
+                transpose_prior(2, new_bank("prior_bank2", "t0"))
+                transpose_prior(3, new_bank("prior_bank3", "h1"))
+                transpose_x(2, "h0")
+            else:
+                transpose_prior(i + 3, bank)
+            transpose_r(i, bank)
             if i == 0:
                 copy_prior(2)
             if 0 < i and i + 3 < LATE:
                 widen_x(i + 3)
-            if LATE <= i + 3 < NT:
+            if LATE <= i + 3:
                 sort_x(i + 3)
-            if i < NT:
-                relu_r(i)
-            if 3 < i < 6:
-                relu_h(i - 2)
-                finish_gate(i - 2)
-            if i + 3 < NT:
-                copy_prior(i + 3)
-            if 0 < i < NT:
-                both_halves(matmul_t, i - 1)
-            if i == NT:
-                matmul_t(i - 1, 0, "a")
-                matmul_t(i - 1, 1, "x")
+            relu_r(i)
+            copy_prior(i + 3)
             if i > 0:
+                both_halves(matmul_t, i - 1)
                 both_halves(sigmoid_t, i - 1)
-            if i + 1 < NT:
-                matmul_a(i + 1)
+            matmul_a(i + 1)
             if i < 2:
                 matmul_h(0, i)
             else:
                 both_halves(matmul_h, i - 1)
-            if i + 2 < NT:
-                scale_x(i + 2)
-            if i + 1 < NT:
-                add_bias(i + 1)
-            if i < NT:
-                quantize_r(i)
-            if i + 2 < NT:
+            if i > 2:
+                share_gate(i - 1)
+            scale_x(i + 2)
+            add_bias(i + 1)
+            if i == 4:
+                quantize_x(i + 2)
+            quantize_r(i)
+            if i < 4:
                 quantize_x(i + 2)
             if LATE <= i + 5 < NT:
                 widen_x(i + 5)
-            if i == 4 + 1:
-                gate_and_store(i - 2, 1)
             if i > 0:
-                gate_and_store(i - 1, 0, SHARE if 2 < i <= 4 else 0)
-            if 0 < i and i != 4:
+                gate_and_store(i - 1, 0)
+            if 0 < i < 4:
                 gate_and_store(i - 1, 1)
+        transpose_x(7)
+        transpose_r(5, new_bank("r_bank5", "r"))
+        relu_r(5)
+        matmul_a(6)
+        both_halves(matmul_t, 4)
+        both_halves(sigmoid_t, 4)
+        both_halves(matmul_h, 4)
+        scale_x(7)
+        add_bias_planes(6)
+        quantize_x(7)
+        quantize_r(5)
+        gate_and_store(3, 1)
+        gate_and_store(4, 0)
+        turn_r(6)
+        relu_turned(6)
+        matmul_a(7)
+        both_halves(matmul_t, 5)
+        both_halves(sigmoid_t, 5)
+        both_halves(matmul_h, 5)
+        add_bias_planes(7)
+        gate_and_store(4, 1)
+        quantize_r(6)
+        both_halves(gate_and_store, 5)
+        turn_r(7)
+        relu_turned(7)
+        both_halves(matmul_t, 6)
+        both_halves(sigmoid_t, 6)
+        both_halves(matmul_h, 6)
+        quantize_r(7)
+        both_halves(gate_and_store, 6)
+        matmul_t(7, 0, "a")
+        matmul_t(7, 1, "x")
+        both_halves(sigmoid_t, 7)
+        both_halves(matmul_h, 7)
+        both_halves(gate_and_store, 7)

@@ -267,7 +267,7 @@ def tile_pepnetpriorgatedhiddenlayer_w4_kernel(
             if n + 2 < NT:
                 prior_codes[n + 2], prior_mx_scales[n + 2] = codes[:, P : 2 * P], scales[:, P : 2 * P]
 
-        acc_t, acc_h, gate, result = {}, {}, {}, {}
+        acc_t, acc_h, gate, h_part, pending = {}, {}, {}, {}, {}
 
         def matmul_t(n, j, tag=None):
             acc_t[n, j] = new_bank("acc_t%d_%d" % (n, j), tag or "t%d" % j)
@@ -290,23 +290,24 @@ def tile_pepnetpriorgatedhiddenlayer_w4_kernel(
                     start=(g == 0), stop=(g == 1),
                 )
 
-        def result_tile(n, j):
-            if (n, j) not in result:
-                result[n, j] = work.tile([P, BANK], F32, name="res%d_%d" % (n, j), tag="res", bufs=6)
-            return result[n, j]
-
-        def gate_and_store(n, j):
-            c0 = BANK - SHARE if (n, j) in result else BANK
-            res = result_tile(n, j)
+        def gate_and_store(n, j, shared=0):
+            res = work.tile([P, BANK], F32, name="res%d_%d" % (n, j), tag="res", bufs=6)
+            c0 = BANK - shared
             nc.vector.scalar_tensor_tensor(
                 out=res[:, 0:c0], in0=acc_h[n, j][:, 0:c0], scalar=0.0, in1=gate[n, j][:, 0:c0], op0=ALU.max, op1=ALU.mult
             )
-            nc.sync.dma_start(out=out_rows[:, n, BANK * j : BANK * (j + 1)], in_=res[:])
+            if shared:
+                pending[n] = res
+            else:
+                nc.sync.dma_start(out=out_rows[:, n, BANK * j : BANK * (j + 1)], in_=res[:])
 
-        def share_gate(n):
-            h_part = work.tile([P, SHARE], F32, name="h_part%d" % n, tag="h_part", bufs=2)
-            nc.scalar.activation(out=h_part[:], in_=acc_h[n, 0][:, BANK - SHARE : BANK], func=ACT.Relu)
-            nc.gpsimd.tensor_tensor(out=result_tile(n, 0)[:, BANK - SHARE : BANK], in0=h_part[:], in1=gate[n, 0][:, BANK - SHARE : BANK], op=ALU.mult)
+        def relu_h(n):
+            h_part[n] = work.tile([P, SHARE], F32, name="h_part%d" % n, tag="h_part", bufs=2)
+            nc.scalar.activation(out=h_part[n][:], in_=acc_h[n, 0][:, BANK - SHARE : BANK], func=ACT.Relu)
+
+        def finish_gate(n):
+            nc.gpsimd.tensor_tensor(out=pending[n][:, BANK - SHARE : BANK], in0=h_part[n][:], in1=gate[n, 0][:, BANK - SHARE : BANK], op=ALU.mult)
+            nc.sync.dma_start(out=out_rows[:, n, 0:BANK], in_=pending[n][:])
 
         def keep_tensor_busy(count, tag="a"):
             for i in range(count):
@@ -373,6 +374,9 @@ def tile_pepnetpriorgatedhiddenlayer_w4_kernel(
             if LATE <= i + 3:
                 sort_x(i + 3)
             relu_r(i)
+            if i == 4:
+                relu_h(i - 2)
+                finish_gate(i - 2)
             copy_prior(i + 3)
             if i > 0:
                 both_halves(matmul_t, i - 1)
@@ -382,8 +386,6 @@ def tile_pepnetpriorgatedhiddenlayer_w4_kernel(
                 matmul_h(0, i)
             else:
                 both_halves(matmul_h, i - 1)
-            if i > 2:
-                share_gate(i - 1)
             scale_x(i + 2)
             add_bias(i + 1)
             if i == 4:
@@ -394,20 +396,23 @@ def tile_pepnetpriorgatedhiddenlayer_w4_kernel(
             if LATE <= i + 5 < NT:
                 widen_x(i + 5)
             if i > 0:
-                gate_and_store(i - 1, 0)
+                gate_and_store(i - 1, 0, SHARE if i > 2 else 0)
             if 0 < i < 4:
                 gate_and_store(i - 1, 1)
         transpose_x(7)
         transpose_r(5, new_bank("r_bank5", "r"))
         relu_r(5)
+        scale_x(7)
         matmul_a(6)
         both_halves(matmul_t, 4)
         both_halves(sigmoid_t, 4)
-        both_halves(matmul_h, 4)
-        scale_x(7)
+        matmul_h(4, 0)
+        matmul_h(4, 1, "x")
+        relu_h(3)
         add_bias_planes(6)
         quantize_x(7)
         quantize_r(5)
+        finish_gate(3)
         gate_and_store(3, 1)
         gate_and_store(4, 0)
         turn_r(6)

@@ -37,7 +37,6 @@ def tile_pepnetpriorgatedhiddenlayer_w4_kernel(
         nc.gpsimd.memset(two[:], 2.0)
         ident = keep.tile([P, P], F32, name="ident")
         make_identity(nc, ident[:])
-        ident_bf = keep.tile([P, P], BF16, name="ident_bf")
         twos = keep.tile([P, BANK], BF16, name="twos")
         nc.vector.memset(twos[:], 2.0)
         table_out = keep.tile([P, 1], F32, name="table_out")
@@ -230,21 +229,6 @@ def tile_pepnetpriorgatedhiddenlayer_w4_kernel(
                 out=r_rows[n][:], in0=acc_a[n][:].rearrange("c (p u e) -> c u p e", u=2, e=2), in1=bias[:], op=ALU.add
             )
 
-        def add_bias_planes(n):
-            r_rows[n] = work.tile([P, 4, P], BF16, name="r_rows%d" % n, tag="r_rows", bufs=2)
-            nc.vector.tensor_tensor(
-                out=r_rows[n][:].rearrange("c (u e) p -> c u e p", e=2), in0=acc_a[n][:].rearrange("c (p u e) -> c u e p", u=2, e=2),
-                in1=bias[:].rearrange("c u p e -> c u e p"), op=ALU.add,
-            )
-
-        def turn_r(n):
-            r_t[n] = psum.tile([P, 4, P], F32, name="r_turned%d" % n, tag="r")
-            for m in range(4):
-                nc.tensor.matmul(r_t[n][:, m, :], r_rows[n][:, m, :], ident_bf[:], start=True, stop=True)
-
-        def relu_turned(n):
-            nc.scalar.activation(out=joint_tile(n)[:, 0:512].rearrange("p (c m) -> p c m", m=4), in_=r_t[n][:].rearrange("p m c -> p c m"), func=ACT.Relu)
-
         def transpose_r(n, bank):
             r_t[n] = bank[:, 256:512]
             words = r_rows[n][:].rearrange("c u p e -> c (u p e)").bitcast(F32)
@@ -333,7 +317,6 @@ def tile_pepnetpriorgatedhiddenlayer_w4_kernel(
         wl.append(load_words("wl1", wl_words[:, :, 2 * BANK : 4 * BANK]))
         load_x(6, 8)
         load_prior(6, 8)
-        nc.scalar.copy(out=ident_bf[:], in_=ident[:])
         widen_x(1)
         spread = spread_bias()
         transpose_prior(0, new_bank("prior_bank0", "r"))
@@ -409,24 +392,24 @@ def tile_pepnetpriorgatedhiddenlayer_w4_kernel(
         matmul_h(4, 0)
         matmul_h(4, 1, "x")
         relu_h(3)
-        add_bias_planes(6)
+        add_bias(6)
         quantize_x(7)
         quantize_r(5)
         finish_gate(3)
         gate_and_store(3, 1)
         gate_and_store(4, 0)
-        turn_r(6)
-        relu_turned(6)
+        transpose_r(6, new_bank("r_bank6", "r"))
+        relu_r(6)
         matmul_a(7)
         both_halves(matmul_t, 5)
         both_halves(sigmoid_t, 5)
         both_halves(matmul_h, 5)
-        add_bias_planes(7)
+        add_bias(7)
         gate_and_store(4, 1)
         quantize_r(6)
         both_halves(gate_and_store, 5)
-        turn_r(7)
-        relu_turned(7)
+        transpose_r(7, new_bank("r_bank7", "r"))
+        relu_r(7)
         both_halves(matmul_t, 6)
         both_halves(sigmoid_t, 6)
         both_halves(matmul_h, 6)

@@ -6,7 +6,7 @@ from concourse.masks import make_identity
 P = 128
 TOKENS, D, PRIOR, G, HID = 1024, 1024, 512, 512, 1024
 NT = TOKENS // P
-LATE = 6
+LATE = 5
 SHARE = 256
 BANK = 512
 FLOPS = 2 * TOKENS * (D * G + PRIOR * G + G * HID + D * HID)
@@ -113,7 +113,8 @@ def tile_pepnetpriorgatedhiddenlayer_w4_kernel(
 
         def joint_tile(n):
             if n not in joint:
-                joint[n] = work.tile([P, 2 * P * 4], BF16, name="joint%d" % n, tag="joint", bufs=3, align_bytes=64)
+                late = LATE <= n + 5 < NT
+                joint[n] = work.tile([P, 2 * P * 4], BF16, name="joint%d" % n, tag="x_late%d" % (n + 5) if late else "joint", bufs=1 if late else 3, align_bytes=64)
             return joint[n]
 
         prior_t, prior_grouped, prior_codes, prior_mx_scales = {}, {}, {}, {}
@@ -164,8 +165,7 @@ def tile_pepnetpriorgatedhiddenlayer_w4_kernel(
                     nc.tensor.transpose(x_t[n][:, u, g, :], cols, ident[:])
 
         def new_x_tiles(n):
-            tag = "x_late%d" % (n + 3) if LATE <= n + 3 < NT else "x_grouped"
-            x_grouped[n] = work.tile([P, 2 * P * 4], BF16, name="x_grouped%d" % n, tag=tag, bufs=1 if LATE <= n + 3 < NT else 2, align_bytes=64)
+            x_grouped[n] = work.tile([P, 2 * P * 4], BF16, name="x_grouped%d" % n, tag="x_grouped", bufs=2, align_bytes=64)
             x_codes[n] = keep.tile([P, 2 * P], U32, name="x_codes%d" % n, align_bytes=64)
             x_mx_scales[n] = keep.tile([P, 2 * P], U8, name="x_mx_scales%d" % n, align_bytes=64)
 
@@ -361,21 +361,18 @@ def tile_pepnetpriorgatedhiddenlayer_w4_kernel(
                 relu_h(i - 2)
                 finish_gate(i - 2)
             copy_prior(i + 3)
+            matmul_a(i + 1)
             if i > 0:
                 both_halves(matmul_t, i - 1)
                 both_halves(sigmoid_t, i - 1)
-            matmul_a(i + 1)
             if i < 2:
                 matmul_h(0, i)
             else:
                 both_halves(matmul_h, i - 1)
             scale_x(i + 2)
             add_bias(i + 1)
-            if i == 4:
-                quantize_x(i + 2)
+            quantize_x(i + 2)
             quantize_r(i)
-            if i < 4:
-                quantize_x(i + 2)
             if LATE <= i + 5 < NT:
                 widen_x(i + 5)
             if i > 0:

@@ -36,8 +36,7 @@ def tile_pepnetpriorgatedhiddenlayer_w4_kernel(
         two = keep.tile([P, 1], F32, name="two")
         nc.gpsimd.memset(two[:], 2.0)
         ident = keep.tile([P, P], F32, name="ident")
-        make_identity(nc, ident[:])
-        twos = keep.tile([P, BANK], BF16, name="twos")
+        twos = keep.tile([P, P], BF16, name="twos")
         nc.vector.memset(twos[:], 2.0)
         table_out = keep.tile([P, 1], F32, name="table_out")
         nc.scalar.activation(out=table_out[:], in_=two[:], func=ACT.Sigmoid)
@@ -48,6 +47,8 @@ def tile_pepnetpriorgatedhiddenlayer_w4_kernel(
         wl_sc = keep.tile([P, 2, HID], U8, name="wl_sc", align_bytes=64)
         nc.vector.memset(b_row[:], 0.0)
         nc.vector.memset(a_scales[:].rearrange("p c n -> p (c n)").bitcast(I32), 0)
+        nc.vector.memset(ident[:], 0.0)
+        make_identity(nc, ident[:], nomemset=True)
         nc.vector.memset(wl_sc[:].rearrange("p c n -> p (c n)").bitcast(I32), 0)
 
         x_rows = x_bytes.rearrange("(p n) k -> p n k", n=NT)
@@ -93,18 +94,21 @@ def tile_pepnetpriorgatedhiddenlayer_w4_kernel(
         load_x(3, 4)
 
         s_twice = keep.tile([P, 2, 4], F32, name="s_twice")
-        bias = keep.tile([P, 2, P, 2], F32, name="bias")
+        bias = keep.tile([P, 2, P, 2], BF16, name="bias")
 
         def double_scales():
             nc.vector.tensor_scalar(out=s_twice[:], in0=s_col[:], scalar1=2.0, scalar2=None, op0=ALU.mult)
 
         def spread_bias():
-            spread = new_bank("spread", "t0")
-            nc.tensor.matmul(spread[:], twos[:, 0:P], b_row[:], start=True, stop=True)
+            spread = psum.tile([P, G], BF16, name="spread", tag="t0")
+            nc.tensor.matmul(spread[:], twos[:], b_row[:], start=True, stop=True)
             return spread
 
         def copy_bias(spread):
-            nc.scalar.copy(out=bias[:], in_=spread[:].rearrange("c (p u e) -> c u p e", u=2, e=2))
+            nc.scalar.copy(
+                out=bias[:].rearrange("c u p e -> c (u p e)").bitcast(F32).rearrange("c (u p) -> c u p", u=2),
+                in_=spread[:].bitcast(F32).rearrange("c (p u) -> c u p", u=2),
+            )
 
         def new_bank(name, tag):
             return psum.tile([P, BANK], F32, name=name, tag=tag)
@@ -296,7 +300,7 @@ def tile_pepnetpriorgatedhiddenlayer_w4_kernel(
         def keep_tensor_busy(count, tag="a"):
             for i in range(count):
                 junk = new_bank("junk", tag)
-                nc.tensor.matmul(junk[:], twos[:, 0:P], twos[:], start=True, stop=True)
+                nc.tensor.matmul(junk[:].rearrange("p (a b) -> p a b", a=4), twos[:], twos[:].unsqueeze(1).to_broadcast([P, 4, P]), start=True, stop=True)
 
         def both_halves(stage, n):
             for j in range(2):
@@ -311,9 +315,9 @@ def tile_pepnetpriorgatedhiddenlayer_w4_kernel(
         load_scales(wl_sc, wl_scales)
         wl = [load_words("wl0", wl_words[:, :, 0 : 2 * BANK])]
         load_prior(4, 6)
+        load_x(4, 6)
         load_scales(w2_sc, w2_scales)
         w2 = load_words("w2", w2_words)
-        load_x(4, 6)
         wl.append(load_words("wl1", wl_words[:, :, 2 * BANK : 4 * BANK]))
         load_x(6, 8)
         load_prior(6, 8)
@@ -392,9 +396,9 @@ def tile_pepnetpriorgatedhiddenlayer_w4_kernel(
         add_bias(6)
         quantize_x(7)
         quantize_r(5)
-        finish_gate(3)
         gate_and_store(3, 1)
         gate_and_store(4, 0)
+        finish_gate(3)
         transpose_r(6, new_bank("r_bank6", "r"))
         relu_r(6)
         matmul_a(7)

@@ -8,6 +8,7 @@ TOKENS, D, PRIOR, G, HID = 1024, 1024, 512, 512, 1024
 NT = TOKENS // P
 LATE = 5
 SHARE = 256
+FIRST_LATE = 768
 BANK = 512
 FLOPS = 2 * TOKENS * (D * G + PRIOR * G + G * HID + D * HID)
 
@@ -81,9 +82,9 @@ def tile_pepnetpriorgatedhiddenlayer_w4_kernel(
             return words
 
         load_x(0, 1)
+        load_x(1, 3)
         s_col = keep.tile([P, 2, 4], F32, name="s_col")
         nc.sync.dma_start(out=s_col[:], in_=x_scale.rearrange("o (g p m) -> p (o g) m", g=2, m=4))
-        load_x(1, 3)
         load_prior(0, 2)
         nc.sync.dma_start(out=b_row[0:1, :], in_=b1.rearrange("(o n) -> o n", o=1))
         load_scales(a_scales[:, 1:3, :], wx_scales)
@@ -123,11 +124,18 @@ def tile_pepnetpriorgatedhiddenlayer_w4_kernel(
 
         prior_t, prior_grouped, prior_codes, prior_mx_scales = {}, {}, {}, {}
 
+        prior_sorted = {}
+
+        def sort_prior(n):
+            prior_sorted[n] = keep.tile([P, 2, P], F32, name="prior_sorted%d" % n)
+            nc.scalar.copy(out=prior_sorted[n][:], in_=prior_in[n].bitcast(F32).rearrange("c (p u) -> c u p", u=2))
+
         def transpose_prior(n, bank):
             prior_t[n] = bank[:, 0:256].rearrange("p (u r) -> p u r", u=2)
             words = prior_in[n].bitcast(F32)
             for u in range(2):
-                nc.tensor.transpose(prior_t[n][:, u, :], words[:, u : 256 : 2], ident[:])
+                cols = prior_sorted[n][:, u, :] if n in prior_sorted else words[:, u : 256 : 2]
+                nc.tensor.transpose(prior_t[n][:, u, :], cols, ident[:])
 
         def copy_prior(n):
             if n < 2:
@@ -154,7 +162,8 @@ def tile_pepnetpriorgatedhiddenlayer_w4_kernel(
                 nc.scalar.copy(out=x_wide[n][:], in_=x_fp8[n])
             else:
                 x_wide[n] = work.tile([P, D], BF16, name="x_wide%d" % n, tag="x_late%d" % n, bufs=1, align_bytes=64)
-                nc.gpsimd.tensor_copy(out=x_wide[n][:], in_=x_fp8[n])
+                c1 = FIRST_LATE if n == LATE else D
+                nc.gpsimd.tensor_copy(out=x_wide[n][:, 0:c1], in_=x_fp8[n][:, 0:c1])
 
         def sort_x(n):
             x_sorted[n] = work.tile([P, 2, 2, P], F32, name="x_sorted%d" % n, tag="x_sorted", bufs=2)
@@ -323,12 +332,12 @@ def tile_pepnetpriorgatedhiddenlayer_w4_kernel(
         load_prior(6, 8)
         widen_x(1)
         spread = spread_bias()
+        copy_bias(spread)
         transpose_prior(0, new_bank("prior_bank0", "r"))
         copy_prior(0)
         transpose_prior(1, new_bank("prior_bank1", "t1"))
         keep_tensor_busy(1)
         transpose_x(1)
-        copy_bias(spread)
         widen_x(2)
         copy_prior(1)
         widen_x(3)
@@ -348,9 +357,9 @@ def tile_pepnetpriorgatedhiddenlayer_w4_kernel(
                 transpose_x(i + 2)
             bank = new_bank("r_bank%d" % i, "r")
             if i == 0:
+                transpose_x(2, "h0")
                 transpose_prior(2, new_bank("prior_bank2", "t0"))
                 transpose_prior(3, new_bank("prior_bank3", "h1"))
-                transpose_x(2, "h0")
             else:
                 transpose_prior(i + 3, bank)
             transpose_r(i, bank)
@@ -358,8 +367,11 @@ def tile_pepnetpriorgatedhiddenlayer_w4_kernel(
                 copy_prior(2)
             if 0 < i and i + 3 < LATE:
                 widen_x(i + 3)
+                nc.scalar.copy(out=x_wide[LATE][:, FIRST_LATE:D], in_=x_fp8[LATE][:, FIRST_LATE:D])
             if LATE <= i + 3:
                 sort_x(i + 3)
+            if i in (2, 3):
+                sort_prior(i + 4)
             relu_r(i)
             if i == 4:
                 relu_h(i - 2)

from contextlib import ExitStack

import concourse.mybir as mybir
from concourse.masks import make_identity

P = 128
TOKENS, D, PRIOR, G, HID = 1024, 1024, 512, 512, 1024
NT = TOKENS // P
LATE = 5
SHARE = 256
FIRST_LATE = 768
BANK = 512
FLOPS = 2 * TOKENS * (D * G + PRIOR * G + G * HID + D * HID)

F32 = mybir.dt.float32
BF16 = mybir.dt.bfloat16
I32 = mybir.dt.int32
U32 = mybir.dt.uint32
U8 = mybir.dt.uint8
FP8 = mybir.dt.float8_e4m3fn
FP8X4 = mybir.dt.float8_e4m3fn_x4
FP4X4 = mybir.dt.float4_e2m1fn_x4
ACT = mybir.ActivationFunctionType
ALU = mybir.AluOpType


def tile_pepnetpriorgatedhiddenlayer_w4_kernel(
    tc, x_bytes, x_scale, prior, wx_words, wx_scales, wp_words, wp_scales, b1, w2_words, w2_scales, wl_words, wl_scales, out
):
    nc = tc.nc
    with ExitStack() as ctx:
        keep = ctx.enter_context(tc.tile_pool(name="keep", bufs=1))
        work = ctx.enter_context(tc.tile_pool(name="work", bufs=3))
        psum = ctx.enter_context(tc.psum_pool(name="psum", bufs=1))
        ctx.enter_context(tc.manual_schedule())

        two = keep.tile([P, 1], F32, name="two")
        nc.gpsimd.memset(two[:], 2.0)
        ident = keep.tile([P, P], F32, name="ident")
        twos = keep.tile([P, P], BF16, name="twos")
        nc.vector.memset(twos[:], 2.0)
        table_out = keep.tile([P, 1], F32, name="table_out")
        nc.scalar.activation(out=table_out[:], in_=two[:], func=ACT.Sigmoid)
        b_row = keep.tile([P, G], BF16, name="b_row")

        a_scales = keep.tile([P, 3, G], U8, name="a_scales", align_bytes=64)
        w2_sc = keep.tile([P, 1, HID], U8, name="w2_sc", align_bytes=64)
        wl_sc = keep.tile([P, 2, HID], U8, name="wl_sc", align_bytes=64)
        nc.vector.memset(b_row[:], 0.0)
        nc.vector.memset(a_scales[:].rearrange("p c n -> p (c n)").bitcast(I32), 0)
        nc.vector.memset(ident[:], 0.0)
        make_identity(nc, ident[:], nomemset=True)
        nc.vector.memset(wl_sc[:].rearrange("p c n -> p (c n)").bitcast(I32), 0)

        x_rows = x_bytes.rearrange("(p n) k -> p n k", n=NT)
        prior_rows = prior.rearrange("(p n) k -> p n k", n=NT)
        out_rows = out.rearrange("(p n) h -> p n h", n=NT)
        x_fp8, prior_in = {}, {}

        def load_x(n0, n1):
            rows = keep.tile([P, n1 - n0, D], U8, name="x_fp8_%d" % n0)
            nc.sync.dma_start(out=rows[:], in_=x_rows[:, n0:n1, :])
            for n in range(n0, n1):
                x_fp8[n] = rows[:, n - n0, :].bitcast(FP8)

        def load_prior(n0, n1):
            rows = keep.tile([P, (n1 - n0) * PRIOR], BF16, name="prior_in_%d" % n0)
            nc.sync.dma_start(out=rows[:], in_=prior_rows[:, n0:n1, :].rearrange("p n k -> p (n k)"))
            for n in range(n0, n1):
                prior_in[n] = rows[:, (n - n0) * PRIOR : (n - n0 + 1) * PRIOR]

        def load_scales(scale_tile, src):
            for quad in range(4):
                nc.sync.dma_start(
                    out=scale_tile[32 * quad : 32 * quad + 4, :, :].bitcast(I32),
                    in_=src[:, 4 * quad : 4 * quad + 4, :].rearrange("g q n -> q g n").bitcast(I32),
                )

        def load_words(name, src):
            words = keep.tile([P, src.shape[0], src.shape[2]], U8, name=name, align_bytes=64)
            nc.sync.dma_start(out=words[:].bitcast(I32), in_=src.rearrange("g p b -> p g b").bitcast(I32))
            return words

        load_x(0, 1)
        load_x(1, 3)
        s_col = keep.tile([P, 2, 4], F32, name="s_col")
        nc.sync.dma_start(out=s_col[:], in_=x_scale.rearrange("o (g p m) -> p (o g) m", g=2, m=4))
        load_prior(0, 2)
        nc.sync.dma_start(out=b_row[0:1, :], in_=b1.rearrange("(o n) -> o n", o=1))
        load_scales(a_scales[:, 1:3, :], wx_scales)
        wx = load_words("wx", wx_words)
        wp = load_words("wp", wp_words)
        load_scales(a_scales[:, 0:1, :], wp_scales)
        load_prior(2, 4)
        load_x(3, 4)

        s_twice = keep.tile([P, 2, 4], F32, name="s_twice")
        bias = keep.tile([P, 2, P, 2], BF16, name="bias")

        def double_scales():
            nc.vector.tensor_scalar(out=s_twice[:], in0=s_col[:], scalar1=2.0, scalar2=None, op0=ALU.mult)

        def spread_bias():
            spread = psum.tile([P, G], BF16, name="spread", tag="t0")
            nc.tensor.matmul(spread[:], twos[:], b_row[:], start=True, stop=True)
            return spread

        def copy_bias(spread):
            nc.scalar.copy(
                out=bias[:].rearrange("c u p e -> c (u p e)").bitcast(F32).rearrange("c (u p) -> c u p", u=2),
                in_=spread[:].bitcast(F32).rearrange("c (p u) -> c u p", u=2),
            )

        def new_bank(name, tag):
            return psum.tile([P, BANK], F32, name=name, tag=tag)

        joint = {}

        def joint_tile(n):
            if n not in joint:
                late = LATE <= n + 5 < NT
                joint[n] = work.tile([P, 2 * P * 4], BF16, name="joint%d" % n, tag="x_late%d" % (n + 5) if late else "joint", bufs=1 if late else 3, align_bytes=64)
            return joint[n]

        prior_t, prior_grouped, prior_codes, prior_mx_scales = {}, {}, {}, {}

        prior_sorted = {}

        def sort_prior(n):
            prior_sorted[n] = keep.tile([P, 2, P], F32, name="prior_sorted%d" % n)
            nc.scalar.copy(out=prior_sorted[n][:], in_=prior_in[n].bitcast(F32).rearrange("c (p u) -> c u p", u=2))

        def transpose_prior(n, bank):
            prior_t[n] = bank[:, 0:256].rearrange("p (u r) -> p u r", u=2)
            words = prior_in[n].bitcast(F32)
            for u in range(2):
                cols = prior_sorted[n][:, u, :] if n in prior_sorted else words[:, u : 256 : 2]
                nc.tensor.transpose(prior_t[n][:, u, :], cols, ident[:])

        def copy_prior(n):
            if n < 2:
                prior_grouped[n] = work.tile([P, P * 4], BF16, name="prior_grouped%d" % n, tag="prior_grouped", bufs=2, align_bytes=64)[:]
            else:
                prior_grouped[n] = joint_tile(n - 2)[:, 512:1024]
            nc.scalar.activation(
                out=prior_grouped[n].rearrange("p (r u e) -> p r u e", u=2, e=2),
                in_=prior_t[n].rearrange("p u r -> p (u r)").bitcast(BF16).rearrange("p (u r e) -> p r u e", u=2, e=2),
                func=ACT.Copy,
                scale=2.0,
            )

        def quantize_prior(n):
            prior_codes[n] = keep.tile([P, P], U32, name="prior_codes%d" % n, align_bytes=64)
            prior_mx_scales[n] = keep.tile([P, P], U8, name="prior_mx_scales%d" % n, align_bytes=64)
            nc.vector.quantize_mx(out=prior_codes[n][:].bitcast(FP8X4), scales=prior_mx_scales[n][:], in_=prior_grouped[n])

        x_wide, x_sorted, x_t, x_grouped, x_codes, x_mx_scales = {}, {}, {}, {}, {}, {}

        def widen_x(n):
            if n < LATE:
                x_wide[n] = work.tile([P, D], BF16, name="x_wide%d" % n, tag="x_wide", bufs=3)
                nc.scalar.copy(out=x_wide[n][:], in_=x_fp8[n])
            else:
                x_wide[n] = work.tile([P, D], BF16, name="x_wide%d" % n, tag="x_late%d" % n, bufs=1, align_bytes=64)
                c1 = FIRST_LATE if n == LATE else D
                nc.gpsimd.tensor_copy(out=x_wide[n][:, 0:c1], in_=x_fp8[n][:, 0:c1])

        def sort_x(n):
            x_sorted[n] = work.tile([P, 2, 2, P], F32, name="x_sorted%d" % n, tag="x_sorted", bufs=2)
            nc.scalar.copy(out=x_sorted[n][:], in_=x_wide[n][:].bitcast(F32).rearrange("c (g p u) -> c g u p", g=2, u=2))

        def transpose_x(n, tag="x"):
            x_t[n] = psum.tile([P, 2, 2, P], F32, name="x_t%d" % n, tag=tag)
            words = x_wide[n][:].bitcast(F32)
            for g in range(2):
                for u in range(2):
                    cols = x_sorted[n][:, g, u, :] if n in x_sorted else words[:, 256 * g + u : 256 * (g + 1) : 2]
                    nc.tensor.transpose(x_t[n][:, u, g, :], cols, ident[:])

        def new_x_tiles(n):
            x_grouped[n] = work.tile([P, 2 * P * 4], BF16, name="x_grouped%d" % n, tag="x_grouped", bufs=2, align_bytes=64)
            x_codes[n] = keep.tile([P, 2 * P], U32, name="x_codes%d" % n, align_bytes=64)
            x_mx_scales[n] = keep.tile([P, 2 * P], U8, name="x_mx_scales%d" % n, align_bytes=64)

        def scale_x(n):
            new_x_tiles(n)
            nc.vector.tensor_tensor(
                out=x_grouped[n][:].rearrange("p (g r u e) -> p g r u e", g=2, u=2, e=2),
                in0=x_t[n][:].rearrange("p u g r -> p (u g r)").bitcast(BF16).rearrange("p (u g r e) -> p g r u e", u=2, g=2, e=2),
                in1=s_twice[:].rearrange("p g (u e) -> p g u e", u=2).unsqueeze(2).to_broadcast([P, 2, P, 2, 2]),
                op=ALU.mult,
            )

        def quantize_x(n):
            nc.vector.quantize_mx(out=x_codes[n][:].bitcast(FP8X4), scales=x_mx_scales[n][:], in_=x_grouped[n][:])

        first_wide, first_t = {}, {}

        def widen_first(g):
            first_wide[g] = keep.tile([P, 2, P, 2], BF16, name="first_wide%d" % g)
            nc.vector.tensor_scalar(
                out=first_wide[g][:].rearrange("c u p e -> c p u e"),
                in0=x_fp8[0][:, 512 * g : 512 * (g + 1)].rearrange("c (p u e) -> c p u e", u=2, e=2),
                scalar1=two[:], scalar2=None, op0=ALU.mult,
            )

        def transpose_first(g):
            first_t[g] = psum.tile([P, 2, P], F32, name="first_t%d" % g, tag="h%d" % (g + 1))
            words = first_wide[g][:].rearrange("c u p e -> c (u p e)").bitcast(F32)
            for u in range(2):
                nc.tensor.transpose(first_t[g][:, u, :], words[:, P * u : P * (u + 1)], ident[:])

        def scale_first(g):
            nc.vector.tensor_tensor(
                out=x_grouped[0][:, 512 * g : 512 * (g + 1)].rearrange("p (r u e) -> p r u e", u=2, e=2),
                in0=first_t[g][:].rearrange("p u r -> p (u r)").bitcast(BF16).rearrange("p (u r e) -> p r u e", u=2, e=2),
                in1=s_col[:, g, :].rearrange("p (u e) -> p u e", u=2).unsqueeze(1).to_broadcast([P, P, 2, 2]),
                op=ALU.mult,
            )

        def quantize_first(g):
            nc.vector.quantize_mx(
                out=x_codes[0][:, P * g : P * (g + 1)].bitcast(FP8X4), scales=x_mx_scales[0][:, P * g : P * (g + 1)],
                in_=x_grouped[0][:, 512 * g : 512 * (g + 1)],
            )

        acc_a, r_rows, r_t, r_codes, r_mx_scales = {}, {}, {}, {}, {}

        def matmul_a(n):
            acc_a[n] = psum.tile([P, G], F32, name="acc_a%d" % n, tag="a")
            passes = [(x_codes[n][:, P * g : P * (g + 1)], x_mx_scales[n][:, P * g : P * (g + 1)], wx[:, g, :], a_scales[:, 1 + g, :]) for g in range(2)]
            passes.append((prior_codes[n][:], prior_mx_scales[n][:], wp[:, 0, :], a_scales[:, 0, :]))
            for i, (codes, scales, w, w_scales) in enumerate(passes):
                nc.tensor.matmul_mx(
                    out=acc_a[n][:], lhsT=codes.bitcast(FP8X4), lhsT_scale=scales, rhs=w.bitcast(FP4X4),
                    rhs_scale=w_scales, start=(i == 0), stop=(i == 2),
                )

        def add_bias(n):
            r_rows[n] = work.tile([P, 2, P, 2], BF16, name="r_rows%d" % n, tag="r_rows", bufs=2)
            nc.vector.tensor_tensor(
                out=r_rows[n][:], in0=acc_a[n][:].rearrange("c (p u e) -> c u p e", u=2, e=2), in1=bias[:], op=ALU.add
            )

        def transpose_r(n, bank):
            r_t[n] = bank[:, 256:512]
            words = r_rows[n][:].rearrange("c u p e -> c (u p e)").bitcast(F32)
            for u in range(2):
                nc.tensor.transpose(r_t[n][:, P * u : P * (u + 1)], words[:, P * u : P * (u + 1)], ident[:])

        def relu_r(n):
            nc.scalar.activation(
                out=joint_tile(n)[:, 0:512].rearrange("p (c u e) -> p c u e", u=2, e=2),
                in_=r_t[n].bitcast(BF16).rearrange("p (u c e) -> p c u e", u=2, e=2),
                func=ACT.Relu,
            )

        def quantize_r(n):
            width = 2 * P if n + 2 < NT else P
            codes = keep.tile([P, width], U32, name="r_codes%d" % n, align_bytes=64)
            scales = keep.tile([P, width], U8, name="r_mx_scales%d" % n, align_bytes=64)
            nc.vector.quantize_mx(out=codes[:].bitcast(FP8X4), scales=scales[:], in_=joint[n][:, 0 : 4 * width])
            r_codes[n], r_mx_scales[n] = codes[:, 0:P], scales[:, 0:P]
            if n + 2 < NT:
                prior_codes[n + 2], prior_mx_scales[n + 2] = codes[:, P : 2 * P], scales[:, P : 2 * P]

        acc_t, acc_h, gate, h_part, pending = {}, {}, {}, {}, {}

        def matmul_t(n, j, tag=None):
            acc_t[n, j] = new_bank("acc_t%d_%d" % (n, j), tag or "t%d" % j)
            nc.tensor.matmul_mx(
                out=acc_t[n, j][:], lhsT=r_codes[n][:].bitcast(FP8X4), lhsT_scale=r_mx_scales[n][:],
                rhs=w2[:, 0, 2 * BANK * j : 2 * BANK * (j + 1)].bitcast(FP4X4), rhs_scale=w2_sc[:, 0, BANK * j : BANK * (j + 1)],
                start=True, stop=True,
            )

        def sigmoid_t(n, j):
            gate[n, j] = work.tile([P, BANK], F32, name="gate%d_%d" % (n, j), tag="gate", bufs=4)
            nc.scalar.activation(out=gate[n, j][:], in_=acc_t[n, j][:], func=ACT.Sigmoid, scale=0.5)

        def matmul_h(n, j, tag=None):
            acc_h[n, j] = new_bank("acc_h%d_%d" % (n, j), tag or "h%d" % ((2 * n + j + 2) % 3))
            for g in range(2):
                nc.tensor.matmul_mx(
                    out=acc_h[n, j][:], lhsT=x_codes[n][:, P * g : P * (g + 1)].bitcast(FP8X4), lhsT_scale=x_mx_scales[n][:, P * g : P * (g + 1)],
                    rhs=wl[j][:, g, :].bitcast(FP4X4), rhs_scale=wl_sc[:, g, BANK * j : BANK * (j + 1)],
                    start=(g == 0), stop=(g == 1),
                )

        def gate_and_store(n, j, shared=0):
            res = work.tile([P, BANK], F32, name="res%d_%d" % (n, j), tag="res", bufs=6)
            c0 = BANK - shared
            nc.vector.scalar_tensor_tensor(
                out=res[:, 0:c0], in0=acc_h[n, j][:, 0:c0], scalar=0.0, in1=gate[n, j][:, 0:c0], op0=ALU.max, op1=ALU.mult
            )
            if shared:
                pending[n] = res
            else:
                nc.sync.dma_start(out=out_rows[:, n, BANK * j : BANK * (j + 1)], in_=res[:])

        def relu_h(n):
            h_part[n] = work.tile([P, SHARE], F32, name="h_part%d" % n, tag="h_part", bufs=2)
            nc.scalar.activation(out=h_part[n][:], in_=acc_h[n, 0][:, BANK - SHARE : BANK], func=ACT.Relu)

        def finish_gate(n):
            nc.gpsimd.tensor_tensor(out=pending[n][:, BANK - SHARE : BANK], in0=h_part[n][:], in1=gate[n, 0][:, BANK - SHARE : BANK], op=ALU.mult)
            nc.sync.dma_start(out=out_rows[:, n, 0:BANK], in_=pending[n][:])

        def keep_tensor_busy(count, tag="a"):
            for i in range(count):
                junk = new_bank("junk", tag)
                nc.tensor.matmul(junk[:].rearrange("p (a b) -> p a b", a=4), twos[:], twos[:].unsqueeze(1).to_broadcast([P, 4, P]), start=True, stop=True)

        def both_halves(stage, n):
            for j in range(2):
                stage(n, j)

        keep_tensor_busy(3)
        for g in range(2):
            widen_first(g)
            transpose_first(g)
        double_scales()
        nc.vector.memset(w2_sc[:].rearrange("p c n -> p (c n)").bitcast(I32), 0)
        load_scales(wl_sc, wl_scales)
        wl = [load_words("wl0", wl_words[:, :, 0 : 2 * BANK])]
        load_prior(4, 6)
        load_x(4, 6)
        load_scales(w2_sc, w2_scales)
        w2 = load_words("w2", w2_words)
        wl.append(load_words("wl1", wl_words[:, :, 2 * BANK : 4 * BANK]))
        load_x(6, 8)
        load_prior(6, 8)
        widen_x(1)
        spread = spread_bias()
        copy_bias(spread)
        transpose_prior(0, new_bank("prior_bank0", "r"))
        copy_prior(0)
        transpose_prior(1, new_bank("prior_bank1", "t1"))
        keep_tensor_busy(1)
        transpose_x(1)
        widen_x(2)
        copy_prior(1)
        widen_x(3)
        new_x_tiles(0)
        for g in range(2):
            scale_first(g)
        quantize_first(0)
        quantize_first(1)
        quantize_prior(0)
        scale_x(1)
        matmul_a(0)
        add_bias(0)
        quantize_x(1)
        quantize_prior(1)
        for i in range(NT - 3):
            if i > 0:
                transpose_x(i + 2)
            bank = new_bank("r_bank%d" % i, "r")
            if i == 0:
                transpose_x(2, "h0")
                transpose_prior(2, new_bank("prior_bank2", "t0"))
                transpose_prior(3, new_bank("prior_bank3", "h1"))
            else:
                transpose_prior(i + 3, bank)
            transpose_r(i, bank)
            if i == 0:
                copy_prior(2)
            if 0 < i and i + 3 < LATE:
                widen_x(i + 3)
                nc.scalar.copy(out=x_wide[LATE][:, FIRST_LATE:D], in_=x_fp8[LATE][:, FIRST_LATE:D])
            if LATE <= i + 3:
                sort_x(i + 3)
            if i in (2, 3):
                sort_prior(i + 4)
            relu_r(i)
            if i == 4:
                relu_h(i - 2)
                finish_gate(i - 2)
            copy_prior(i + 3)
            matmul_a(i + 1)
            if i > 0:
                both_halves(matmul_t, i - 1)
                both_halves(sigmoid_t, i - 1)
            if i < 2:
                matmul_h(0, i)
            else:
                both_halves(matmul_h, i - 1)
            scale_x(i + 2)
            add_bias(i + 1)
            quantize_x(i + 2)
            quantize_r(i)
            if LATE <= i + 5 < NT:
                widen_x(i + 5)
            if i > 0:
                gate_and_store(i - 1, 0, SHARE if i > 2 else 0)
            if 0 < i < 4:
                gate_and_store(i - 1, 1)
        transpose_x(7)
        transpose_r(5, new_bank("r_bank5", "r"))
        relu_r(5)
        scale_x(7)
        matmul_a(6)
        both_halves(matmul_t, 4)
        both_halves(sigmoid_t, 4)
        matmul_h(4, 0)
        matmul_h(4, 1, "x")
        relu_h(3)
        add_bias(6)
        quantize_x(7)
        quantize_r(5)
        gate_and_store(3, 1)
        gate_and_store(4, 0)
        finish_gate(3)
        transpose_r(6, new_bank("r_bank6", "r"))
        relu_r(6)
        matmul_a(7)
        both_halves(matmul_t, 5)
        both_halves(sigmoid_t, 5)
        both_halves(matmul_h, 5)
        add_bias(7)
        gate_and_store(4, 1)
        quantize_r(6)
        both_halves(gate_and_store, 5)
        transpose_r(7, new_bank("r_bank7", "r"))
        relu_r(7)
        both_halves(matmul_t, 6)
        both_halves(sigmoid_t, 6)
        both_halves(matmul_h, 6)
        quantize_r(7)
        both_halves(gate_and_store, 6)
        matmul_t(7, 0, "a")
        matmul_t(7, 1, "x")
        both_halves(sigmoid_t, 7)
        both_halves(matmul_h, 7)
        both_halves(gate_and_store, 7)
